import numpy as np, ml_dtypes
CORES = [48,51,52,55]
N = 4
BF = ml_dtypes.bfloat16
def gentries(a):
    return np.ascontiguousarray(a.reshape(8, 16, -1).transpose(0, 2, 1)).reshape(8, -1)
def gtable(e):
    e = np.asarray(e); return np.ascontiguousarray(e.reshape(8, -1, 16).transpose(0, 2, 1)).reshape(128, -1).astype(np.int32)
W, NB, R, H = 4096, 16, 4, 1
KAP = (101, 1303, 2717, 3911)
def spot(u, l):
    return ((u * u >> 5) + 37 * u + KAP[l]) & (W - 1)
def figures(x, n):
    return np.take_along_axis(x, n.reshape(8, 1, -1), 2).reshape((8, 16) + n.shape[1:])
def witness(x, w, F):
    w = w.reshape(8, 16, 1, 1, 1)
    for l in range(4):
        h = F.shape[3] >> 1
        a, b = F[:, :, :, 0::2], F[:, :, :, 1::2]
        u = np.add.reduce(w * np.abs(a - b), axis=1) & (W - 1)
        F = figures(x, spot(u, l))
    return F[:, :, :, 0]
def judge(x, w, n):
    F = figures(x, n)
    col = witness(x, w, F); row = witness(x, w, F.transpose(0, 1, 2, 4, 3))
    return col, np.add.reduce(np.abs(col - row), axis=1), np.add.reduce(col, axis=1), np.add.reduce(row, axis=1)
def readings(x, w, n):
    x8 = np.broadcast_to(x, (8, 16, W)); w8 = np.broadcast_to(w, (8, 16))
    return np.ascontiguousarray(witness(x8, w8, figures(x8, n.reshape(8, -1, 16, 1)))[..., 0].transpose(1, 0, 2)).reshape(16, -1)
def parts(rng):
    x = rng.integers(0, 256, (N, 8, 16, W)); w = rng.integers(0, 256, (N, 8, 16)); th = rng.integers(800, 2000, (N, 8, 16))
    return x, w, th, rng.integers(0, W, (N, 8, NB * 256)), rng.integers(0, W, (N, 8, NB * 256))
def pack(x, w, th, b, c):
    return {"xf": np.ascontiguousarray(x.reshape(N, 128, W)).astype(np.float32).astype(BF), "bn": np.stack([gtable(a) for a in b]), "cn": np.stack([gtable(a) for a in c]),
            "wt": np.ascontiguousarray(w.reshape(N, 128, 1)).astype(np.int32), "th": np.ascontiguousarray(th.reshape(N, 128, 1)).astype(np.int32)}
def setup_inputs(rng):
    return pack(*parts(rng))
def setup_inputs_spread(rng):
    x, w, th, b, c = parts(rng)
    s = np.exp2(8.5 * rng.random((N, 8, 1, W))) * (rng.random((N, 8, 1, W)) > 0.0625)
    x = np.minimum((s * rng.random((N, 8, 16, W))).astype(np.int64), 255)
    w = np.minimum(np.exp2(8 * rng.random((N, 8, 16))).astype(np.int64) - rng.integers(0, 2, (N, 8, 16)), 255)
    th = np.minimum(np.exp2(11 * rng.random((N, 8, 16))).astype(np.int64), 4080)
    b = np.minimum((W * rng.random(b.shape) ** 3).astype(np.int64), W - 1); c = np.minimum((W * rng.random(c.shape) ** 2).astype(np.int64), W - 1)
    b[:, 1::2] = W - 1 - b[:, 1::2]; c[:, ::3] = W - 1 - c[:, ::3]
    return pack(x, w, th, b, c)
def setup_inputs_ends(rng):
    x = 255 * rng.integers(0, 2, (N, 8, 16, W)); w = 255 * rng.integers(0, 2, (N, 8, 16)); th = 4080 * rng.integers(0, 2, (N, 8, 16))
    w[:, 0, 0] = 0; w[:, 0, 15] = 255; th[:, 0, 0] = 0; th[:, 0, 15] = 4080
    b, c = [np.where(rng.random((N, 8, NB * 256)) < 0.8, (W - 1) * rng.integers(0, 2, (N, 8, NB * 256)), rng.integers(0, W, (N, 8, NB * 256))) for i in range(2)]
    for g in (2, 5, 7):
        x[:, g] = 255 * rng.integers(0, 2, (N, 1, W)); w[:, g] = 255
    for q in range(0, N - 1, 2): w[q, 7, q] = 0
    for q in range(N):
        for g in (2, 5, 7):
            u = 255 * int(np.add.reduce(w[q, g])) & (W - 1)
            x[q, g, :, 0] = 0; x[q, g, :, W - 1] = 255
            for l in range(4): x[q, g, :, spot(0, l)] = 0
            for l in range(4): x[q, g, :, spot(u, l)] = 255
    bb = b.reshape(N, 8, NB, 16, 16)
    bb[:, 7, :, :, 0] = 0; bb[:, 7, NB - 1] = 0; bb[:, 7, NB - 1, 0, 15] = W - 1; bb[:, 7, NB - 1, 1, 0] = W - 1
    th[:, 7, 15] = 0; th[N - 1, 7, 15] = 4080
    return pack(x, w, th, bb.reshape(N, 8, NB * 256), c)
def setup_inputs_corners(rng):
    x, w, th, b, c = parts(rng)
    for q in range(N):
        for g in range(8):
            k = (g + q) % 8
            if k == 0: w[q, g] = 0
            if k == 1: w[q, g] = 255
            if k == 2: w[q, g] = 16 * rng.integers(1, 16, 16); th[q, g] = 0
            if k == 3: th[q, g] = 4080
            if k == 4: b[q, g] = np.repeat(rng.choice(np.array([0, 1, W - 1, W >> 1]), NB), 256); c[q, g] = rng.permutation(NB * 256) % W
            if k == 5: b[q, g] = np.arange(NB * 256) % W; c[q, g] = W - 1 - b[q, g]
            if k == 6: w[q, g] = 0; w[q, g, 15] = 255
            if k == 7: x[q, g] = 255 * rng.integers(0, 2, (1, W))
    return pack(x, w, th, b, c)
def setup_inputs_full(rng):
    x, w, th, b, c = parts(rng); bb = b.reshape(N, 8, NB, 16, 16); z = spot(0, 3)
    for q in range(N):
        for g in range(8):
            k = (g + q) % 8
            if k < 4: th[q, g] = rng.integers(0, 256, 16)
            if k < 3:
                w[q, g, 0] |= 1; x[q, g, :, z] = rng.integers(240, 256, 16)
                n = rng.integers(0, W, (512, 16)); f = readings(x[q, g], w[q, g], n)
                s = np.add.reduce(f, axis=0); d = np.add.reduce(w[q, g][:, None] * f, axis=0) & (NB - 1)
                for v, p in enumerate(rng.permutation(NB)):
                    turn = k == 1 or (k == 2 and p % 2 == 1)
                    i = int(np.argmax(np.where(d == v, -s if turn else s, -5000)))
                    bb[q, g, p] = n[i][:, None] if turn else rng.integers(0, W, (1, 16))
                    bb[q, g, p, :, 0] = n[i]
            if k == 3:
                w[q, g] = 255; x[q, g, :, z] = 255; x[q, g, rng.permutation(16)[:2 + q], z] = 254
                bb[q, g, :, :, 0] = rng.integers(0, W, (NB, 1))
            if k == 4: x[q, g] = rng.integers(235, 256, (16, W)); w[q, g] = rng.integers(253, 256, 16)
            if k == 7: x[q, g] = rng.integers(246, 256, (16, W)); w[q, g] = rng.integers(240, 256, 16)
            if k == 5 or k == 6:
                e = int(rng.choice(np.array([8, 24, 60, 90])))
                x[q, g] = np.abs(255 * rng.integers(0, 2, (1, W)) - rng.integers(0, e + 1, (16, W))); w[q, g] = rng.integers(240, 256, 16)
        col, D, A, E = judge(x[q], w[q], bb[q])
        i = np.argmax(np.where(D >= 2304, rng.random(D.shape), -1.0), axis=1)
        t = np.take_along_axis(D - (A & 15), i[:, None, :], 1)[:, 0] - rng.integers(0, 2, (8, 16))
        for g in range(8):
            k = (g + q) % 8
            if k > 3: th[q, g] = np.minimum(np.maximum(t[g], 0), 4080)
            if k == 4 or k == 7: th[q, g, ::2] = rng.integers(0, 16, 8)
    return pack(x, w, th, bb.reshape(N, 8, NB * 256), c)
def setup_inputs_ties(rng):
    x, w, th, b, c = parts(rng)
    base = rng.integers(0, 256, (N, 16, 1)); order = np.argsort(rng.random((N, 16, W)), axis=1)
    x[:, 6] = np.take_along_axis(np.ascontiguousarray(np.broadcast_to(base, (N, 16, W))), order, 1)
    x[:, 4, :, 1::2] = x[:, 4, :, 0::2]
    bb = b.reshape(N, 8, NB, 16, 16)
    s = bb[:, 1, ::3].copy(); bb[:, 1, ::3] = np.triu(s) + np.swapaxes(np.triu(s, 1), -1, -2)
    bb[:, 2, :, :, 0] = bb[:, 2, :1, :, 0].copy()
    for q in range(N):
        col, D, A, E = judge(x[q], w[q], bb[q])
        v = np.take_along_axis(D - (A & 15), rng.integers(0, NB, (8, 1, 16)), 1)[:, 0]
        th[q] = np.minimum(np.maximum(v + rng.choice(np.array([-1, 0, 0, 1]), (8, 16)), 0), 4080)
    th[:, 6, 1::2] = 0
    return pack(x, w, th, bb.reshape(N, 8, NB * 256), c)
def check_inputs(d):
    bad = []
    for k, lo, hi in (("xf", 0, 255), ("bn", 0, W - 1), ("cn", 0, W - 1), ("wt", 0, 255), ("th", 0, 4080)):
        v = np.asarray(d[k]).astype(np.float64)
        if not (np.min(v) >= lo and np.max(v) <= hi): bad.append("range of " + k)
        if np.any(v != np.floor(v)): bad.append("whole numbers of " + k)
    return bad
def reference(xf, bn, cn, wt, th):
    x = np.asarray(xf).astype(np.float32).astype(np.int64).reshape(N, 8, 16, W); w = wt.astype(np.int64).reshape(N, 8, 16); lim = th.astype(np.int64).reshape(N, 8, 16)
    b = np.stack([gentries(a) for a in bn]).astype(np.int64).reshape(N, 8, NB, 16, 16)
    c = np.stack([gentries(a) for a in cn]).astype(np.int64).reshape(N, 8, NB, 16, 16)
    cnt = np.zeros((N, 8, NB, 16), np.int64); low = np.tril(np.ones((NB, NB), bool), -1)
    for t in range(R):
        for a in range(N):
            q = (a - H * t) % N
            col, D, A, E = judge(x[a], w[a], b[q])
            qr = D > lim[a][:, None, :] + (A & 15); cnt[a] += qr
            d = np.add.reduce(w[a][:, :, None] * col[:, :, :, 0], axis=1) & (NB - 1)
            act = ~np.any((d[:, :, None] == d[:, None, :]) & low, axis=2)
            for g in range(8):
                for k in np.flatnonzero(act[g]):
                    one, two = b[q, g, k], c[a, g, d[g, k]]
                    j = np.flatnonzero(qr[g, k] & (A[g, k] <= E[g, k])); v = one[:, j]; one[:, j] = two[:, j]; two[:, j] = v
                    j = np.flatnonzero(qr[g, k] & (A[g, k] > E[g, k])); v = one[j]; one[j] = two[j]; two[j] = v
    yb = np.stack([gtable(b[(a - H * (R - 1)) % N].reshape(8, -1)) for a in range(N)]); yc = np.stack([gtable(e.reshape(8, -1)) for e in c])
    return {"yb": yb.astype(np.float32), "yc": yc.astype(np.float32), "yq": np.ascontiguousarray(cnt.transpose(0, 1, 3, 2)).reshape(N, 128, NB).astype(np.float32)}

@@ -1,0 +1,500 @@
+from concourse.bass import DstId, RemoteDMATransfer
+from concourse.mybir import dt, AluOpType, ActivationFunctionType
+
+A = AluOpType
+AF = ActivationFunctionType
+ROUNDS = 4
+KAP = (101, 1303, 2717, 3911)
+BF, F32, I32, U16 = "bfloat16", "float32", "int32", "uint16"
+
+SCRATCH = {
+    "xx": ("sbuf", [128, 8192], BF),
+    "wti": ("sbuf", [128, 1], I32), "thi": ("sbuf", [128, 1], I32), "wf": ("sbuf", [128, 1], F32),
+    "pid": ("sbuf", [128, 3], I32),
+    "j16": ("sbuf", [128, 1], F32), "j8": ("sbuf", [128, 3], F32),
+    "ones": ("sbuf", [128, 128], F32), "ms1": ("sbuf", [128, 128], F32), "bl": ("sbuf", [128, 128], F32),
+    "cm": ("sbuf", [128, 2, 16], F32), "thp": ("sbuf", [128, 2], I32), "thq": ("sbuf", [128, 2], F32),
+    "dth": ("sbuf", [128, 2, 128], BF), "onb": ("sbuf", [128, 8], BF),
+    "idn": ("sbuf", [128, 128], F32), "nid": ("sbuf", [128, 128], F32), "idb": ("sbuf", [128, 128], BF),
+    "wz": ("sbuf", [128, 144], BF), "uz": ("sbuf", [128, 144], BF), "wb": ("sbuf", [128, 128], BF),
+    "w2z": ("sbuf", [128, 144], BF), "nwz": ("sbuf", [128, 144], BF),
+    "pf": ("sbuf", [128, 128], F32), "cf": ("sbuf", [128, 128], F32),
+    "sel": ("sbuf", [128, 3, 128], BF), "exl": ("sbuf", [128, 40], U16),
+    "rs": ("sbuf", [128, 9], F32),
+    "raw": ("sbuf", [128, 4, 8, 16], I32),
+    "ch": ("sbuf", [128, 2, 132], F32),
+    "yqs": ("sbuf", [128, 16], F32),
+    "qr": ("sbuf", [128, 4, 16], BF),
+    "roc": ("sbuf", [128, 2, 8, 16], F32),
+}
+for _h in range(2):
+    for _n, _s, _d in (
+            ("f0", [128, 2, 512], BF), ("d0", [128, 4, 512], BF), ("z0", [128, 4, 512], BF),
+            ("f1", [128, 2, 512], BF), ("d1", [128, 2, 512], BF), ("z1", [128, 2, 512], BF),
+            ("f2", [128, 512], BF), ("d2", [128, 512], BF),
+            ("f3", [128, 384], BF), ("d3c", [128, 128], BF), ("d3r", [128, 128], BF), ("a3", [128, 2, 2, 2, 32], BF),
+            ("q3", [128, 3, 128], BF),
+            ("nl", [128, 240], U16),
+            ("ivc", [128, 4, 64], I32), ("ivr", [128, 4, 64], I32), ("iv1", [128, 4, 64], I32),
+            ("iv2", [128, 5, 32], I32), ("iv3", [128, 5, 16], I32),
+            ("mc", [128, 32, 2], I32), ("mr", [128, 4, 2, 8], I32), ("m1", [128, 4, 2, 8], I32),
+            ("si", [128, 64], I32), ("sf", [128, 48], F32),
+            ("oh", [128, 9], F32), ("cu", [128, 9], F32),
+            ("lt", [128, 256], F32), ("ltt", [128, 256], F32), ("ly", [128, 384], BF),
+            ("bf", [128, 132], F32), ("xm", [128, 128], F32), ("dl", [128, 128], F32), ("b2", [128, 128], F32),
+            ("rob", [128, 8, 16], F32),
+            ("lb", [128, 4, 128], U16), ("sn", [128, 3, 128], U16)):
+        SCRATCH[_n + str(_h)] = ("sbuf", _s, _d)
+    for _b in range(4):
+        SCRATCH["ps%d%d" % (_h, _b)] = ("psum", [128, 512], F32)
+SEMAPHORES = ["eV", "eS", "eP", "eG", "snd", "lxa", "lxb", "lw", "lth", "lr0", "lr1", "lr2", "lr3", "ost"]
+SEMAPHORES += ["rc%d%d" % (_t, _h) for _t in range(1, ROUNDS) for _h in range(2)]
+
+ABS0 = "SSSS"
+ABS1 = "SS"
+GEST = 1.5
+BIAS = 100.0
+TUNE = {}
+
+
+def house(k):
+    return (k & 7) << 1 | k >> 3
+
+
+def build(g, core, T, topo):
+    rank = T.rank_of(core)
+    dst = T.cores[(rank + 1) % len(T.cores)]
+    V, S, P = g.vector, g.scalar, g.tensor
+    ops = []
+    cur = [0, None]
+    lastw, readers = {}, {}
+
+    def op(q, fns, r=(), w=(), cost=0.1, grp=None, sem=None, lat=0.0):
+        deps = set()
+        for k in r:
+            if k in lastw:
+                deps.update(lastw[k])
+        for k in w:
+            if k in lastw:
+                deps.update(lastw[k])
+            deps.update(readers.get(k, ()))
+        i = len(ops)
+        for k in w:
+            lastw[k] = [i]
+            readers[k] = []
+        for k in r:
+            if k not in w:
+                readers.setdefault(k, []).append(i)
+        if cur[1] is not None:
+            cur[1] += 1
+        ops.append({"b": cur[0], "k": (cur[0] % 2, cur[1]), "q": q, "f": fns, "d": sorted(deps), "c": cost, "grp": grp, "lat": lat, "sem": sem})
+        return i
+
+    def v(fn, r, w, n, per=1.0):
+        return op("V", [fn], r, w, 0.001 * max(64, n * per) + 0.02)
+
+    def vg(fn, r, w, n):
+        return op("V", [fn], r, w, 0.05 + 0.001 * GEST * n)
+
+    def s(fn, r, w, n, per=1.0):
+        return op("S", [fn], r, w, 0.06 + 0.001 * per * n)
+
+    def pe(fns, r, w, n, per=1.0):
+        return op("P", fns, r, w, len(fns) * max(64, n) * 0.0007 * per + 0.03)
+
+    def gc(fn, r, w, n):
+        return op("G", [fn], r, w, 0.15 + 0.002 * n)
+
+    def load(q, out, in_, w, grp, r=(), lat=2.2):
+        eng = {"Y": g.sync, "S": g.scalar}[q]
+        return op(q, [lambda: eng.dma_start(out, in_)], r, w, 0.08, grp, lat=lat)
+
+    def first(lat, *a):
+        ops[load(*a, lat=lat)]["first"] = 1e6 - len(ops)
+
+    def beta(c):
+        return (c & 1) << 2 | (c & 6) >> 1
+
+    first(5.5, "Y", T.xx[:, 0:4096], T.xf[:], ["xa"], "lxa")
+    for c in range(8):
+        first(3.0, "S", T.raw[:, 0, beta(c), :], T.bn[c::8, 0:128], ["raw0_%d" % c], "lr0")
+    first(3.0, "Y", T.wti[:], T.wt[:], ["wti"], "lw")
+    for c in range(8):
+        first(7.0, "Y", T.raw[:, 1, beta(c), :], T.bn[c::8, 128:256], ["raw1_%d" % c], "lr1")
+    first(9.0, "Y", T.xx[:, 4096:4096 + 3920], T.xf[:, 0:3920], ["xb"], "lxb")
+    first(9.0, "Y", T.thi[:], T.th[:], ["thi"], "lth")
+    for c in range(16):
+        first(11.0, "Y", T.raw[:, 2 + c // 8, beta(c), :], T.cn[c::16, :], ["raw%d_%d" % (2 + c // 8, c % 8)], "lr%d" % (2 + c // 8))
+
+    gc(lambda: g.iota(T.pid[:, 0:1], [[0, 1]], 0, 1), [], ["pid0"], 1)
+    v(lambda: V.memset(T.ones[:], 1.0), [], ["ones"], 128)
+    gc(lambda: g.affine_select(T.ms1[:], T.ones[:], [[-16, 8], [0, 16]], A.is_ge, 0.0, 0, 1), ["ones"], ["ms1b"], 128)
+    gc(lambda: g.affine_select(T.bl[:], T.ms1[:], [[16, 8], [0, 16]], A.is_ge, 0.0, 15, -1), ["ms1b"], ["bl"], 128)
+    gc(lambda: g.affine_select(T.cm[:, 1, :], T.ones[:, 0:16], [[-8, 2], [-16, 8]], A.is_ge, 0.0, 0, 1), ["ones"], ["cm1"], 16)
+    gc(lambda: g.affine_select(T.cm[:, 0, :], T.cm[:, 1, :], [[8, 2], [16, 8]], A.is_ge, 0.0, 7, -1), ["cm1"], ["cm0"], 16)
+    gc(lambda: g.affine_select(T.idn[:], T.ones[:], [[-1, 128]], A.is_equal, 0.0, 0, 1), ["ones"], ["idn"], 128)
+    gc(lambda: g.iota(T.pf[:], [[1, 2], [0, 8], [2, 8]], 0, 0, allow_small_or_imprecise_dtypes=True), [], ["pf"], 128)
+    for p0 in range(2):
+        for c0 in range(2):
+            o = 64 * p0 + 32 * c0
+            gc(lambda o=o, c0=c0: g.iota(T.cf[:, o:o + 32], [[4, 2], [2, 2], [0, 8]], c0, 0, allow_small_or_imprecise_dtypes=True), [], ["cf%d" % o], 32)
+    for z in ("wz", "uz", "w2z", "nwz"):
+        if z in ("w2z", "nwz") and "V" not in ABS0 + ABS1:
+            continue
+        v(lambda z=z: V.memset(T[z][:], 0.0), [], [z], 144, 0.5)
+    v(lambda: V.tensor_copy(T.wf[:], T.wti[:]), ["wti"], ["wf"], 1)
+    v(lambda: V.tensor_scalar(T.wz[:, 15:143:16], T.bl[:, 0:128:16], T.wf[:, 0:1], None, A.mult), ["bl", "wf", "wz"], ["wz"], 8)
+    if "V" in ABS0 + ABS1:
+        v(lambda: V.tensor_scalar(T.w2z[:, 15:143:16], T.bl[:, 0:128:16], T.wf[:, 0:1], 2.0, A.mult, A.mult), ["bl", "wf"], ["w2z"], 8)
+        v(lambda: V.tensor_scalar(T.nwz[:, 15:143:16], T.bl[:, 0:128:16], T.wf[:, 0:1], -1.0, A.mult, A.mult), ["bl", "wf"], ["nwz"], 8)
+    v(lambda: V.tensor_scalar(T.uz[:, 15:143:16], T.bl[:, 0:128:16], 1.0, None, A.mult), ["bl"], ["uz"], 8)
+    v(lambda: V.tensor_scalar(T.wb[:], T.bl[:], T.wf[:, 0:1], None, A.mult), ["bl", "wf"], ["wb"], 128)
+    v(lambda: V.tensor_scalar(T.nid[:], T.idn[:], -1.0, None, A.mult), ["idn"], ["nid"], 128)
+    v(lambda: V.tensor_copy(T.idb[:], T.idn[:]), ["idn"], ["idb"], 128)
+    v(lambda: V.tensor_scalar(T.pid[:, 1:2], T.pid[:, 0:1], 15, None, A.bitwise_and), ["pid0"], ["pid1"], 1)
+    v(lambda: V.tensor_scalar(T.pid[:, 2:3], T.pid[:, 0:1], 7, None, A.bitwise_and), ["pid0"], ["pid2"], 1)
+    v(lambda: V.tensor_copy(T.j16[:], T.pid[:, 1:2]), ["pid1"], ["j16"], 1)
+    v(lambda: V.tensor_scalar(T.j8[:, 0:1], T.pid[:, 2:3], 8.0, None, A.subtract), ["pid2"], ["j8a"], 1)
+    v(lambda: V.tensor_scalar(T.j8[:, 1:2], T.pid[:, 2:3], 16.0, None, A.subtract), ["pid2"], ["j8b"], 1)
+    cfs = ["cf0", "cf32", "cf64", "cf96"]
+    for k in range(2):
+        v(lambda k=k: V.tensor_scalar(T.sel[:, k, :], T.cf[:], 8.0 * k, T.j16[:, 0:1], A.add, A.is_equal), cfs + ["j16"], ["sel%d" % k], 128)
+    v(lambda: V.tensor_scalar(T.sel[:, 2, :], T.pf[:], T.j16[:, 0:1], None, A.is_equal), ["pf", "j16"], ["sel2"], 128)
+    v(lambda: V.tensor_scalar(T.exl[:, 0:16], T.cm[:, 0, :], T.j8[:, 0:1], 8.0, A.mult, A.add), ["cm0", "j8a"], ["exl"], 16)
+    v(lambda: V.tensor_scalar(T.exl[:, 16:32], T.cm[:, 0, :], T.j8[:, 1:2], 16.0, A.mult, A.add), ["cm0", "j8b"], ["exy0"], 16)
+    v(lambda: V.tensor_scalar(T.exl[:, 32:40], T.bl[:, 0:128:16], T.j8[:, 0:1], 16.0, A.mult, A.add), ["bl", "j8a"], ["exy1"], 8)
+    for h in range(2):
+        v(lambda h=h: V.memset(T["sf%d" % h][:], 0.0), [], ["sfz%d" % h], 48)
+    v(lambda: V.tensor_scalar(T.thp[:, 0:1], T.thi[:], 4080, None, A.bitwise_and), ["thi"], ["thp0"], 1)
+    v(lambda: V.tensor_scalar(T.thp[:, 1:2], T.thi[:], 15, None, A.bitwise_and), ["thi"], ["thp1"], 1)
+    v(lambda: V.tensor_scalar(T.thq[:], T.thp[:], -1.0, None, A.mult), ["thp0", "thp1"], ["thq"], 2)
+    for k in range(2):
+        v(lambda k=k: V.tensor_scalar(T.dth[:, k, :], T.idn[:], T.thq[:, k:k + 1], None, A.mult), ["idn", "thq"], ["dth%d" % k], 128)
+    v(lambda: V.memset(T.onb[:], 1.0), [], ["onb"], 8)
+    v(lambda: V.memset(T.rs[:], 1.0), [], ["rs"], 9)
+    v(lambda: V.memset(T.oh0[:], 0.0), [], ["oh0", "ohc0"], 9)
+    v(lambda: V.memset(T.bf0[:, 128:132], 0.0), [], ["bfz0"], 4)
+    v(lambda: V.memset(T.bf1[:, 128:132], 0.0), [], ["bfz1"], 4)
+    v(lambda: V.memset(T.ch[:, :, 128:132], 1.0), [], ["chz"], 8)
+
+    def fromraw(x, outs, wname):
+        rr = ["raw%d_%d" % (x, c) for c in range(8)]
+        for qd in range(4):
+            p0, c0 = qd >> 1, qd & 1
+            v(lambda qd=qd, p0=p0, c0=c0: V.tensor_copy(outs(qd), T.raw[:, x, 4 * c0:4 * c0 + 4, p0::2]), rr, [wname % qd], 32)
+
+    def half(t, h):
+        H = str(h)
+        cur[0] = 2 * t + h
+
+        def n(*a):
+            return [x + "@" + H for x in a]
+
+        def tb(name):
+            return T[name + H]
+        ps = [T["ps%d%d" % (h, b)] for b in range(4)]
+        ne = len(engs)
+        win0 = T.xx[:, 0:4096]
+        win = T.xx[:, 0:8192]
+        lb = tb("lb")
+        nl = tb("nl")
+        if t == 0:
+            fromraw(h, lambda qd: lb[:, 0, 32 * qd:32 * qd + 32], "lb0%d_" % h + "%d")
+            if h == 0:
+                for k in range(2):
+                    fromraw(2 + k, lambda qd, k=k: T.ch[:, k, 32 * qd:32 * qd + 32], "chi%d_" % k + "%d")
+        LB = ["lb%d%d_%d" % (t, h, qd) for qd in range(4)]
+        cur[1] = 0
+
+        f0, d0, z0 = tb("f0"), tb("d0"), tb("z0")
+        cm = {}
+        for piece, qd in ((0, 0), (1, 3)):
+            s(lambda piece=piece, qd=qd: S.activation(f0[:, piece, :], win0.indirect(lb[:, t, 32 * qd:32 * qd + 32]), AF.Copy),
+              ["xa", LB[qd]], n("f0_%d" % piece), 512, GEST)
+        for reg, qd, piece in ((0, 2, 0), (2, 1, 0), (1, 1, 1), (3, 2, 1)):
+            vg(lambda reg=reg, qd=qd, piece=piece: V.tensor_tensor(d0[:, reg, :], win0.indirect(lb[:, t, 32 * qd:32 * qd + 32]), f0[:, piece, :], A.subtract),
+               ["xa", LB[qd]] + n("f0_%d" % piece), n("d0_%d" % reg), 512)
+
+        def absol(kind, d, z, key):
+            if kind == "S":
+                s(lambda: S.activation(d, d, AF.Abs), n(key), n(key), 512)
+            else:
+                v(lambda: V.tensor_scalar(z, d, 0.0, None, A.max), n(key), n("z" + key), 512, 0.5)
+
+        for reg in range(4):
+            absol(ABS0[reg], d0[:, reg, :], z0[:, reg, :], "d0_%d" % reg)
+
+        def wsum(out, parts, bank, keys, per_r, to=lambda r: r):
+            fns = []
+            tot = 16 * len(parts)
+            k = 0
+            for lz, f in parts:
+                for r in range(16):
+                    fns.append(lambda lz=lz, f=f, r=r, k=k: P.matmul(out, T[lz][:, 15 - to(r):143 - to(r)], f(r), k == 0, k == tot - 1))
+                    k += 1
+            pe(fns, [p[0] for p in parts] + keys, n(bank), per_r)
+
+        def parts_of(kind, dd, zz):
+            if kind == "S":
+                return [("wz", dd)]
+            return [("w2z", zz), ("nwz", dd)]
+
+        def zk(kind, *keys):
+            return n(*keys) + (n(*["z" + k for k in keys]) if kind == "V" else [])
+
+        def index(iv, src, bank, m, mkey, nn):
+            i = mkey
+            tmp = ps[int(bank[2])][:, 384:384 + nn]
+            v(lambda: V.tensor_copy(iv[:, 0, :], src), [], n(bank, i + "0"), nn)
+            v(lambda: V.tensor_scalar(iv[:, 1, :], iv[:, 0, :], 4095, None, A.bitwise_and), n(i + "0"), n(i + "1"), nn)
+            v(lambda: V.tensor_scalar(tmp, iv[:, 1, :], 1184, None, A.add), n(i + "1"), n(bank), nn)
+            v(lambda: V.tensor_tensor(iv[:, 3, :], iv[:, 1, :], tmp, A.mult), n(i + "1"), n(bank, i + "3"), nn)
+            v(lambda: V.tensor_scalar(m, iv[:, 3, :], 5, 4095, A.arith_shift_right, A.bitwise_and), n(i + "3"), n(i), nn)
+
+        def tolist(out, in_, k, mkey, w, nn):
+            v(lambda: V.tensor_scalar(out, in_, KAP[k], None, A.add), n(mkey), n(w), nn)
+
+        for a, b, kk in ((0, 2, "c"), (2, 4, "r")):
+            bank = "ps0" if kk == "c" else "ps1"
+            out = ps[0][:, 0:64] if kk == "c" else ps[1][:, 0:64]
+            wsum(out, parts_of(ABS0[a], lambda r, a=a, b=b: d0[:, a:b, r::16], lambda r, a=a, b=b: z0[:, a:b, r::16]),
+                 bank, zk(ABS0[a], "d0_%d" % a, "d0_%d" % (a + 1)), 64)
+            m = tb("m" + kk)
+            index(tb("iv" + kk), out, bank, m[:], "m" + kk, 64)
+            if kk == "c":
+                tolist(nl[:, 0:32], m[:, :, 0], 0, "mc", "n1ec", 32)
+                tolist(nl[:, 64:96], m[:, :, 1], 0, "mc", "n1oc", 32)
+            else:
+                tolist(nl[:, 32:64], m[:, :, 0, :], 0, "mr", "n1er", 32)
+                tolist(nl[:, 96:128], m[:, :, 1, :], 0, "mr", "n1or", 32)
+        f1, d1, z1 = tb("f1"), tb("d1"), tb("z1")
+        for y, kk in ((0, "c"), (1, "r")):
+            s(lambda y=y: S.activation(f1[:, y, :], win.indirect(nl[:, 32 * y:32 * y + 32]), AF.Copy),
+              ["xa", "xb"] + n("n1e" + kk), n("f1" + kk), 512, GEST)
+            vg(lambda y=y: V.tensor_tensor(d1[:, y, :], win.indirect(nl[:, 64 + 32 * y:96 + 32 * y]), f1[:, y, :], A.subtract),
+               ["xa", "xb"] + n("n1o" + kk, "f1" + kk), n("d1" + kk), 512)
+            absol(ABS1[y], d1[:, y, :], z1[:, y, :], "d1" + kk)
+        wsum(ps[2][:, 0:64], parts_of(ABS1[0], lambda r: d1[:, :, r::16], lambda r: z1[:, :, r::16]), "ps2", zk(ABS1[0], "d1c", "d1r"), 64)
+        m1 = tb("m1")
+        index(tb("iv1"), ps[2][:, 0:64], "ps2", m1[:], "m1", 64)
+        tolist(nl[:, 128:144], m1[:, 0:2, :, 0::2], 1, "m1", "n2ec", 16)
+        tolist(nl[:, 144:160], m1[:, 2:4, 0, :], 1, "m1", "n2er", 16)
+        tolist(nl[:, 160:176], m1[:, 0:2, :, 1::2], 1, "m1", "n2oc", 16)
+        tolist(nl[:, 176:192], m1[:, 2:4, 1, :], 1, "m1", "n2or", 16)
+        f2, d2 = tb("f2"), tb("d2")
+        s(lambda: S.activation(f2[:], win.indirect(nl[:, 128:160]), AF.Copy), ["xa", "xb"] + n("n2ec", "n2er"), n("f2"), 512, GEST)
+        vg(lambda: V.tensor_tensor(d2[:], win.indirect(nl[:, 160:192]), f2[:], A.subtract), ["xa", "xb"] + n("n2oc", "n2or", "f2"), n("d2"), 512)
+        s(lambda: S.activation(d2[:], d2[:], AF.Abs), n("d2"), n("d2"), 512)
+        wsum(ps[0][:, 0:32], [("wz", lambda r: d2[:, r::16])], "ps0", n("d2"), 32, lambda r: 2 * (r % 8) + r // 8)
+        iv2 = tb("iv2")
+        index(iv2, ps[0][:, 0:32], "ps0", iv2[:, 4, :], "m2", 32)
+        tolist(nl[:, 200:216], iv2[:, 4, 16:32], 2, "m2", "n3r", 16)
+        tolist(nl[:, 192:200], iv2[:, 4, 0:16:2], 2, "m2", "n3e", 8)
+        tolist(nl[:, 216:224], iv2[:, 4, 1:16:2], 2, "m2", "n3o", 8)
+        f3, d3c, d3r, a3 = tb("f3"), tb("d3c"), tb("d3r"), tb("a3")
+        s(lambda: S.activation(f3[:], win.indirect(nl[:, 192:216]), AF.Copy), ["xa", "xb"] + n("n3e", "n3r"), n("f3"), 384, GEST)
+        vg(lambda: V.tensor_tensor(d3c[:], win.indirect(nl[:, 216:224]), f3[:, 0:128], A.subtract), ["xa", "xb"] + n("n3o", "f3"), n("d3c"), 128)
+        v(lambda: V.tensor_tensor(d3r[:], f3[:, 128:384:2], f3[:, 129:384:2], A.subtract), n("f3"), n("d3r"), 128, 2)
+        for y in range(2):
+            s(lambda y=y: S.activation(a3[:, 0, :, y, :], d3c[:, y:128:2], AF.Abs), n("d3c"), n("a3c%d" % y), 64)
+        s(lambda: S.activation(a3[:, 1, :, :, :], d3r[:], AF.Abs), n("d3r"), n("a3r"), 128)
+        wsum(ps[1][:, 0:16], [("wz", lambda r: a3[:, :, :, :, r::16])], "ps1", n("a3c0", "a3c1", "a3r"), 16)
+        iv3 = tb("iv3")
+        index(iv3, ps[1][:, 0:16], "ps1", iv3[:, 4, :], "m3", 16)
+        tolist(nl[:, 224:240], iv3[:, 4, :], 3, "m3", "n4", 16)
+        q3 = tb("q3")
+        s(lambda: S.activation(q3[:, 0, :], win.indirect(nl[:, 224:232]), AF.Copy), ["xa", "xb"] + n("n4"), n("q30"), 128, GEST)
+        vg(lambda: V.tensor_tensor(q3[:, 1, :], win.indirect(nl[:, 232:240]), q3[:, 0, :], A.subtract), ["xa", "xb"] + n("n4", "q30"), n("q31"), 128)
+        s(lambda: S.activation(q3[:, 2, :], q3[:, 1, :], AF.Abs), n("q31"), n("q32"), 128)
+        si, sf, oh, cu = tb("si"), tb("sf"), tb("oh"), tb("cu")
+        pe([lambda: P.matmul(ps[0][:, 0:8], T.wb[:], q3[:, 0, 0:8], True, True)], ["wb"] + n("q30"), n("ps0"), 8)
+        v(lambda: V.tensor_copy(si[:, 0:8], ps[0][:, 0:8]), [], n("ps0", "di"), 8)
+        v(lambda: V.tensor_scalar(si[:, 16:24], si[:, 0:8], 15, None, A.bitwise_and), n("di"), n("da"), 8)
+        v(lambda: V.tensor_scalar(oh[:, 1:9], si[:, 16:24], T.j16[:, 0:1], None, A.is_equal), ["j16", "oh" + H] + n("da"), n("oh"), 8)
+        v(lambda: V.tensor_tensor_scan(cu[:], T.rs[:], oh[:], 0.0, A.mult, A.max), ["rs", "oh" + H, "ohc" + H] + n("oh"), n("cu"), 9)
+        if h == 0:
+            s(lambda: S.activation(T.oh1[:, 0:1], T.cu0[:, 8:9], AF.Copy), n("cu"), ["ohc1"], 1)
+        v(lambda: V.tensor_tensor(sf[:, 0:8], cu[:, 1:9], cu[:, 0:8], A.subtract), n("cu") + ["sfz" + H], n("fo"), 8, 2)
+        lt, ltt = tb("lt"), tb("ltt")
+        s(lambda: S.activation(lt[:], sf[:, 0:16].indirect(T.exl[:, 0:16]), AF.Copy), ["exl", "sfz" + H] + n("fo"), n("lt"), 256, GEST)
+        fns = []
+        for kap in range(16):
+            r = house(kap)
+            fns.append(lambda kap=kap, r=r: P.matmul(ps[2][:, 0:24], T.uz[:, 15 - r:143 - r], q3[:, :, 8 * kap:8 * kap + 8], kap == 0, False))
+        for k in range(2):
+            fns.append(lambda k=k: P.matmul(ps[2][:, 16:24], T.dth[:, k, :], T.onb[:], False, k == 1))
+        pe(fns, ["uz", "dth0", "dth1", "onb"] + n("q30", "q31", "q32"), n("ps2"), 24)
+        v(lambda: V.tensor_copy(si[:, 32:40], ps[2][:, 0:8]), [], n("ps2", "qi"), 8)
+        v(lambda: V.tensor_scalar(si[:, 56:64], si[:, 32:40], 15, None, A.bitwise_and), n("qi"), n("qa"), 8)
+        v(lambda: V.tensor_scalar(sf[:, 40:48], ps[2][:, 8:16], 0.0, None, A.is_ge), ["sfz" + H], n("ps2", "cw"), 8)
+        qrt = T.qr[:, t, 8 * h:8 * h + 8]
+        v(lambda: V.tensor_tensor(qrt, ps[2][:, 16:24], si[:, 56:64], A.is_gt), n("qa"), n("ps2") + ["qr%d%d" % (t, h)], 8)
+        v(lambda: V.tensor_tensor(sf[:, 16:24], qrt, sf[:, 40:48], A.mult), n("cw") + ["qr%d%d" % (t, h), "sfz" + H], n("mwc"), 8)
+        v(lambda: V.tensor_tensor(sf[:, 24:32], qrt, sf[:, 40:48], A.is_gt), n("cw") + ["qr%d%d" % (t, h), "sfz" + H], n("mwr"), 8)
+        ly = tb("ly")
+        s(lambda: S.activation(ly[:], sf[:, 16:40].indirect(T.exl[:, 16:40]), AF.Copy), ["exy0", "exy1", "sfz" + H] + n("mwc", "mwr"), n("ly"), 384, GEST)
+        bf, xm, dl, b2 = tb("bf"), tb("xm"), tb("dl"), tb("b2")
+        v(lambda: V.tensor_copy(bf[:, 0:128], lb[:, t, :]), LB, n("bf"), 128)
+        bp = ps[0][:, 256:384]
+        s(lambda: S.activation(bp, bf[:, 0:128], AF.Copy), n("bf"), n("ps0"), 128)
+        CH = (["chi%d_%d" % (k, qd) for k in range(2) for qd in range(4)] if t == 0 else []) + ["ch", "chz"]
+        pe([lambda: P.matmul(ps[3][:, 0:129], T.nid[:], bf[:, 0:129], True, False)], ["nid", "bfz" + H] + n("bf"), n("ps3"), 129, 4)
+        pe([lambda k=k: P.matmul(ps[3][:, 0:129], lt[:, 128 * k:128 * k + 128], T.ch[:, k, 0:129], False, k == 1) for k in range(2)],
+           CH + n("lt"), n("ps3"), 129, 4)
+        pe([lambda k=k: P.matmul(ps[1][:, 0:128], ly[:, 128 * k:128 * k + 128], T.sel[:, k, :], k == 0, k == 2) for k in range(3)],
+           ["sel0", "sel1", "sel2"] + n("ly"), n("ps1"), 128)
+        v(lambda: V.tensor_scalar(xm[:], ps[1][:, 0:128], 1.0, ps[3][:, 128:129], A.is_equal, A.mult), [], n("ps1", "ps3", "xm"), 128)
+        v(lambda: V.tensor_tensor(dl[:], ps[3][:, 0:128], xm[:], A.mult), n("xm"), n("ps3", "dl"), 128)
+        if t < ROUNDS - 1:
+            v(lambda: V.tensor_tensor(b2[:], bp, dl[:], A.add), n("dl"), n("ps0", "b2"), 128)
+            sn = tb("sn")
+            v(lambda: V.tensor_copy(sn[:, t, :], b2[:]), n("b2"), n("sn%d" % t), 128)
+            rid, pid = topo.addr(dst)[0:2]
+            msk = sum(1 << e for e in engs)
+            nxt = T["lb" + H][:, t + 1, :]
+            rsem = T.sem["rc%d%d" % (t + 1, h)]
+            op("G", [lambda: g.remote_dma(nxt, sn[:, t, :], rsem, T.sem.snd, pid, rid, msk)],
+               n("sn%d" % t), ["sent%d%d" % (t, h)], 0.3, grp="send")
+            op("N", [], ["sent%d%d" % (t, h)], ["lb%d%d_%d" % (t + 1, h, qd) for qd in range(4)], 2.0, sem=("rc%d%d" % (t + 1, h), ne))
+        else:
+            rob = tb("rob")
+            for qd in range(4):
+                p0, c0 = qd >> 1, qd & 1
+                v(lambda qd=qd, p0=p0, c0=c0: V.tensor_tensor(rob[:, 4 * c0:4 * c0 + 4, p0::2], bp[:, 32 * qd:32 * qd + 32], dl[:, 32 * qd:32 * qd + 32], A.add),
+                  n("dl"), n("ps0", "rob%d" % qd), 32)
+            for c in range(8):
+                q = "YS"[c % 2] if h else "Y"
+                load(q, T.yb[c::8, 128 * h:128 * h + 128], rob[:, beta(c), :], ["yb%d%d" % (h, c)], "ost", n(*["rob%d" % (2 * x + (c & 1)) for x in range(2)]))
+        pe([lambda k=k: P.transpose(ps[2][:, 128 * k:128 * k + 128], lt[:, 128 * k:128 * k + 128], T.idn[:]) for k in range(2)], ["idn"] + n("lt"), n("ps2"), 128, 4)
+        s(lambda: S.activation(ltt[:], ps[2][:, 0:256], AF.Copy), [], n("ps2", "ltt"), 256)
+        if h == 0:
+            return
+        both = [(k, y) for k in range(2) for y in range(2)]
+        pe([lambda k=k, y=y: P.matmul(ps[2][:, 256 + 128 * k:384 + 128 * k], T["ltt%d" % y][:, 128 * k:128 * k + 128], T["dl%d" % y][:], y == 0, y == 1) for k, y in both],
+           ["ltt@0", "dl@0"] + n("ltt", "dl"), n("ps2"), 128, 4)
+        if t < ROUNDS - 1:
+            v(lambda: V.tensor_tensor(T.ch[:, :, 0:128], T.ch[:, :, 0:128], ps[2][:, 256:512], A.subtract),
+              CH, n("ps2") + ["ch"], 256)
+        else:
+            for qd in range(4):
+                p0, c0 = qd >> 1, qd & 1
+                u = [ps[2][:, 256 + 128 * k + 32 * qd:288 + 128 * k + 32 * qd] for k in range(2)]
+                for k in range(2):
+                    v(lambda qd=qd, p0=p0, c0=c0, k=k, u=u: V.tensor_tensor(T.roc[:, k, 4 * c0:4 * c0 + 4, p0::2], T.ch[:, k, 32 * qd:32 * qd + 32], u[k], A.subtract),
+                      CH, n("ps2") + ["roc%d_%d" % (k, qd)], 32)
+            for k in range(2):
+                for c in range(8):
+                    load("YS"[c % 2], T.yc[8 * k + c::16, :], T.roc[:, k, beta(c), :], ["yc%d%d" % (k, c)], "ost", ["roc%d_%d" % (k, 2 * x + (c & 1)) for x in range(2)])
+
+    engs = topo.engines(core, dst)[::2]
+    for t in range(ROUNDS):
+        for h in range(2):
+            half(t, h)
+            cur[1] = None
+    pe([lambda t=t: P.matmul(T.ps00[:, 256:272], T.idb[:], T.qr[:, t, :], t == 0, t == ROUNDS - 1) for t in range(ROUNDS)],
+       ["idb"] + ["qr%d%d" % (t, h) for t in range(ROUNDS) for h in range(2)], ["ps0@0"], 16)
+    s(lambda: S.activation(T.yqs[:], T.ps00[:, 256:272], AF.Copy), [], ["ps0@0", "yqs"], 16)
+    load("Y", T.yq[:], T.yqs[:], ["yq"], "ost", ["yqs"])
+    return ops, engs
+
+
+def schedule(ops):
+    nops = len(ops)
+    succ = [[] for _ in range(nops)]
+    for i, o in enumerate(ops):
+        for d in o["d"]:
+            succ[d].append(i)
+    prio = [0.0] * nops
+    for i in range(nops - 1, -1, -1):
+        o = ops[i]
+        prio[i] = o["c"] + o["lat"] + max([0.03 + prio[j] for j in succ[i]] or [0.0])
+    for i, o in enumerate(ops):
+        prio[i] = o.get("first", prio[i] - BIAS * o["b"] + TUNE.get(o["k"], 0.0))
+    left = [len(o["d"]) for o in ops]
+    ready = [0.0] * nops
+    queues = ("V", "S", "P", "G", "Y", "N")
+    free = {q: 0.0 for q in queues}
+    cand = {q: set() for q in queues}
+    for i in range(nops):
+        if not left[i]:
+            cand[ops[i]["q"]].add(i)
+    order = []
+    while True:
+        best, bq = None, None
+        for q in queues:
+            if cand[q]:
+                st = max(free[q], min(ready[j] for j in cand[q]))
+                if best is None or st < best:
+                    best, bq = st, q
+        if bq is None:
+            return order
+        i = max((j for j in cand[bq] if ready[j] <= best), key=lambda j: prio[j])
+        o = ops[i]
+        cand[bq].remove(i)
+        order.append(i)
+        e = best + o["c"]
+        if bq != "N":
+            free[bq] = e
+        e += o["lat"]
+        o["t"] = (best, e)
+        for j in succ[i]:
+            left[j] -= 1
+            ready[j] = max(ready[j], e + (0.03 if ops[j]["q"] == bq else 0.08))
+            if not left[j]:
+                cand[ops[j]["q"]].add(j)
+
+
+def rank_program(g, core, T, topo):
+    rank = T.rank_of(core)
+    if rank is None:
+        return
+    ops, engs = build(g, core, T, topo)
+    order = schedule(ops)
+    queue = {"V": g.vector, "S": g.scalar, "P": g.tensor, "G": g, "Y": g.sync}
+    total = {}
+    for o in ops:
+        if o["grp"] and o["grp"] != "send":
+            total[o["grp"]] = total.get(o["grp"], 0) + 16
+    known = {q: {} for q in queue}
+    count = {}
+    for i in order:
+        o = ops[i]
+        q = o["q"]
+        if q == "N":
+            o["tok"] = o["sem"]
+            o["clk"] = {}
+            continue
+        kn = known[q]
+        for d in sorted(o["d"], key=lambda d: -order.index(d) if False else -d):
+            tok = ops[d].get("tok")
+            if tok is None:
+                continue
+            if kn.get(tok[0], 0) < tok[1]:
+                queue[q].wait_ge(T.sem[tok[0]], tok[1])
+                kn[tok[0]] = tok[1]
+                for a, b in ops[d]["clk"].items():
+                    if kn.get(a, 0) < b:
+                        kn[a] = b
+        o["clk"] = dict(kn)
+        if o["grp"] == "send":
+            for f in o["f"]:
+                f()
+            o["tok"] = None
+        elif o["grp"]:
+            for f in o["f"]:
+                f().then_inc(T.sem[o["grp"]], 16)
+            o["tok"] = (o["grp"], total[o["grp"]])
+        else:
+            sem = "e" + q
+            for f in o["f"]:
+                f().then_inc(T.sem[sem], 1)
+                count[sem] = count.get(sem, 0) + 1
+            o["tok"] = (sem, count[sem])
+    for sem in sorted(count):
+        g.wait_ge(T.sem[sem], count[sem])
+    for sem in sorted(total):
+        g.wait_ge(T.sem[sem], total[sem])
+    g.wait_ge(T.sem.snd, 2 * (ROUNDS - 1) * len(engs))
+    for t in range(1, ROUNDS):
+        for h in range(2):
+            g.wait_ge(T.sem["rc%d%d" % (t, h)], len(engs))

@@ -15,7 +15,7 @@ SCRATCH = {
     "ones": ("sbuf", [128, 128], F32), "ms1": ("sbuf", [128, 128], F32), "bl": ("sbuf", [128, 128], F32),
     "cm": ("sbuf", [128, 2, 16], F32), "thp": ("sbuf", [128, 2], I32), "thq": ("sbuf", [128, 2], F32),
     "dth": ("sbuf", [128, 2, 128], BF), "onb": ("sbuf", [128, 8], BF),
-    "idn": ("sbuf", [128, 128], F32), "nid": ("sbuf", [128, 128], F32), "idb": ("sbuf", [128, 128], BF),
+    "idn": ("sbuf", [128, 128], F32), "nid": ("sbuf", [128, 128], F32), "idb": ("sbuf", [128, 128], BF), "nib": ("sbuf", [128, 128], BF),
     "wz": ("sbuf", [128, 144], BF), "uz": ("sbuf", [128, 144], BF), "wb": ("sbuf", [128, 128], BF),
     "w2z": ("sbuf", [128, 144], BF), "nwz": ("sbuf", [128, 144], BF),
     "pf": ("sbuf", [128, 128], F32), "cf": ("sbuf", [128, 128], F32),
@@ -51,10 +51,33 @@ SEMAPHORES = ["eV", "eS", "eP", "eG", "snd", "lxa", "lxb", "lw", "lth", "lr0", "
 SEMAPHORES += ["rc%d%d" % (_t, _h) for _t in range(1, ROUNDS) for _h in range(2)]
 
 ABS0 = "SSSS"
+DGATH = "V"
+L0PE = True
+NP1, NP2 = 2, 2
 ABS1 = "SS"
 GEST = 1.5
-BIAS = 100.0
+BIAS = 8.0
+OFFS = 6.0
+AHEAD = 0.15
 TUNE = {}
+
+
+EST = {"cyc": 0.001, "g": 1.7, "pe": 0.0007, "v0": 0.02, "s0": 0.06, "p0": 0.03, "wl": 0.08, "wc": 0.16}
+
+
+def estimate(m, e):
+    kind, n = m
+    if kind == "v":
+        return e["cyc"] * n + e["v0"]
+    if kind == "vg":
+        return 0.05 + e["cyc"] * e["g"] * n
+    if kind == "s":
+        return e["cyc"] * n + e["s0"]
+    if kind == "sg":
+        return 0.065 + e["cyc"] * e["g"] * n
+    if kind == "p":
+        return e["pe"] * n + e["p0"]
+    return n
 
 
 def house(k):
@@ -87,20 +110,22 @@ def build(g, core, T, topo):
                 readers.setdefault(k, []).append(i)
         if cur[1] is not None:
             cur[1] += 1
-        ops.append({"b": cur[0], "k": (cur[0] % 2, cur[1]), "q": q, "f": fns, "d": sorted(deps), "c": cost, "grp": grp, "lat": lat, "sem": sem})
+        m = cost if isinstance(cost, tuple) else ("c", cost)
+        ops.append({"b": cur[0], "k": (cur[0] % 2, cur[1]), "q": q, "f": fns, "d": sorted(deps), "m": m, "c": estimate(m, EST),
+                    "grp": grp, "lat": lat, "sem": sem})
         return i
 
     def v(fn, r, w, n, per=1.0):
-        return op("V", [fn], r, w, 0.001 * max(64, n * per) + 0.02)
+        return op("V", [fn], r, w, ("v", max(64, n * per)))
 
     def vg(fn, r, w, n):
-        return op("V", [fn], r, w, 0.05 + 0.001 * GEST * n)
+        return op("V", [fn], r, w, ("vg", n))
 
     def s(fn, r, w, n, per=1.0):
-        return op("S", [fn], r, w, 0.06 + 0.001 * per * n)
+        return op("S", [fn], r, w, ("sg" if per > 1.0 else "s", n))
 
     def pe(fns, r, w, n, per=1.0):
-        return op("P", fns, r, w, len(fns) * max(64, n) * 0.0007 * per + 0.03)
+        return op("P", fns, r, w, ("p", len(fns) * max(64, n) * per))
 
     def gc(fn, r, w, n):
         return op("G", [fn], r, w, 0.15 + 0.002 * n)
@@ -151,6 +176,7 @@ def build(g, core, T, topo):
     v(lambda: V.tensor_scalar(T.wb[:], T.bl[:], T.wf[:, 0:1], None, A.mult), ["bl", "wf"], ["wb"], 128)
     v(lambda: V.tensor_scalar(T.nid[:], T.idn[:], -1.0, None, A.mult), ["idn"], ["nid"], 128)
     v(lambda: V.tensor_copy(T.idb[:], T.idn[:]), ["idn"], ["idb"], 128)
+    v(lambda: V.tensor_copy(T.nib[:], T.nid[:]), ["nid"], ["nib"], 128)
     v(lambda: V.tensor_scalar(T.pid[:, 1:2], T.pid[:, 0:1], 15, None, A.bitwise_and), ["pid0"], ["pid1"], 1)
     v(lambda: V.tensor_scalar(T.pid[:, 2:3], T.pid[:, 0:1], 7, None, A.bitwise_and), ["pid0"], ["pid2"], 1)
     v(lambda: V.tensor_copy(T.j16[:], T.pid[:, 1:2]), ["pid1"], ["j16"], 1)
@@ -207,22 +233,24 @@ def build(g, core, T, topo):
         cur[1] = 0
 
         f0, d0, z0 = tb("f0"), tb("d0"), tb("z0")
-        cm = {}
-        for piece, qd in ((0, 0), (1, 3)):
-            s(lambda piece=piece, qd=qd: S.activation(f0[:, piece, :], win0.indirect(lb[:, t, 32 * qd:32 * qd + 32]), AF.Copy),
-              ["xa", LB[qd]], n("f0_%d" % piece), 512, GEST)
-        for reg, qd, piece in ((0, 2, 0), (2, 1, 0), (1, 1, 1), (3, 2, 1)):
-            vg(lambda reg=reg, qd=qd, piece=piece: V.tensor_tensor(d0[:, reg, :], win0.indirect(lb[:, t, 32 * qd:32 * qd + 32]), f0[:, piece, :], A.subtract),
-               ["xa", LB[qd]] + n("f0_%d" % piece), n("d0_%d" % reg), 512)
+        s(lambda: S.activation(f0[:, 0, :], win0.indirect(lb[:, t, 0:32]), AF.Copy), ["xa", LB[0]], n("f0_0"), 512, GEST)
+        if DGATH == "V":
+            vg(lambda: V.tensor_copy(f0[:, 1, :], win0.indirect(lb[:, t, 96:128])), ["xa", LB[3]], n("f0_1"), 512)
+        else:
+            s(lambda: S.activation(f0[:, 1, :], win0.indirect(lb[:, t, 96:128]), AF.Copy), ["xa", LB[3]], n("f0_1"), 512, GEST)
+        for reg, qd, y in (((2, 1, 0), (0, 2, 0)) if L0PE else ((2, 1, 0), (0, 2, 0), (1, 1, 1), (3, 2, 1))):
+            vg(lambda reg=reg, qd=qd, y=y: V.tensor_tensor(d0[:, reg, :], win0.indirect(lb[:, t, 32 * qd:32 * qd + 32]), f0[:, y, :], A.subtract),
+               ["xa", LB[qd]] + n("f0_%d" % y), n("d0_%d" % reg), 512)
+        for reg, src, b in (((1, 2, 2), (3, 0, 3)) if L0PE else ()):
+            pe([lambda b=b: P.matmul(ps[b][:, 0:512], T.idb[:], f0[:, 0, :], True, False),
+                lambda b=b: P.matmul(ps[b][:, 0:512], T.nib[:], f0[:, 1, :], False, False),
+                lambda b=b, src=src: P.matmul(ps[b][:, 0:512], T.idb[:], d0[:, src, :], False, True)],
+               ["idb", "nib"] + n("f0_0", "f0_1", "d0_%d" % src), n("ps%d" % b), 512)
 
-        def absol(kind, d, z, key):
-            if kind == "S":
-                s(lambda: S.activation(d, d, AF.Abs), n(key), n(key), 512)
-            else:
-                v(lambda: V.tensor_scalar(z, d, 0.0, None, A.max), n(key), n("z" + key), 512, 0.5)
-
-        for reg in range(4):
-            absol(ABS0[reg], d0[:, reg, :], z0[:, reg, :], "d0_%d" % reg)
+        for reg in ((2, 0) if L0PE else range(4)):
+            s(lambda reg=reg: S.activation(z0[:, reg, :], d0[:, reg, :], AF.Abs), n("d0_%d" % reg), n("z0_%d" % reg), 512)
+        for reg, b in (((1, 2), (3, 3)) if L0PE else ()):
+            s(lambda reg=reg, b=b: S.activation(z0[:, reg, :], ps[b][:, 0:512], AF.Abs), [], n("ps%d" % b, "z0_%d" % reg), 512)
 
         def wsum(out, parts, bank, keys, per_r, to=lambda r: r):
             fns = []
@@ -233,14 +261,6 @@ def build(g, core, T, topo):
                     fns.append(lambda lz=lz, f=f, r=r, k=k: P.matmul(out, T[lz][:, 15 - to(r):143 - to(r)], f(r), k == 0, k == tot - 1))
                     k += 1
             pe(fns, [p[0] for p in parts] + keys, n(bank), per_r)
-
-        def parts_of(kind, dd, zz):
-            if kind == "S":
-                return [("wz", dd)]
-            return [("w2z", zz), ("nwz", dd)]
-
-        def zk(kind, *keys):
-            return n(*keys) + (n(*["z" + k for k in keys]) if kind == "V" else [])
 
         def index(iv, src, bank, m, mkey, nn):
             i = mkey
@@ -257,8 +277,7 @@ def build(g, core, T, topo):
         for a, b, kk in ((0, 2, "c"), (2, 4, "r")):
             bank = "ps0" if kk == "c" else "ps1"
             out = ps[0][:, 0:64] if kk == "c" else ps[1][:, 0:64]
-            wsum(out, parts_of(ABS0[a], lambda r, a=a, b=b: d0[:, a:b, r::16], lambda r, a=a, b=b: z0[:, a:b, r::16]),
-                 bank, zk(ABS0[a], "d0_%d" % a, "d0_%d" % (a + 1)), 64)
+            wsum(out, [("wz", lambda r, a=a, b=b: z0[:, a:b, r::16])], bank, n("z0_%d" % a, "z0_%d" % (a + 1)), 64)
             m = tb("m" + kk)
             index(tb("iv" + kk), out, bank, m[:], "m" + kk, 64)
             if kk == "c":
@@ -269,12 +288,18 @@ def build(g, core, T, topo):
                 tolist(nl[:, 96:128], m[:, :, 1, :], 0, "mr", "n1or", 32)
         f1, d1, z1 = tb("f1"), tb("d1"), tb("z1")
         for y, kk in ((0, "c"), (1, "r")):
-            s(lambda y=y: S.activation(f1[:, y, :], win.indirect(nl[:, 32 * y:32 * y + 32]), AF.Copy),
-              ["xa", "xb"] + n("n1e" + kk), n("f1" + kk), 512, GEST)
-            vg(lambda y=y: V.tensor_tensor(d1[:, y, :], win.indirect(nl[:, 64 + 32 * y:96 + 32 * y]), f1[:, y, :], A.subtract),
-               ["xa", "xb"] + n("n1o" + kk, "f1" + kk), n("d1" + kk), 512)
-            absol(ABS1[y], d1[:, y, :], z1[:, y, :], "d1" + kk)
-        wsum(ps[2][:, 0:64], parts_of(ABS1[0], lambda r: d1[:, :, r::16], lambda r: z1[:, :, r::16]), "ps2", zk(ABS1[0], "d1c", "d1r"), 64)
+            for z in range(NP1):
+                w = 512 // NP1
+                c0, c1, o = z * w, z * w + w, 32 * y + z * w // 16
+                s(lambda y=y, c0=c0, c1=c1, o=o, w=w: S.activation(f1[:, y, c0:c1], win.indirect(nl[:, o:o + w // 16]), AF.Copy),
+                  ["xa", "xb"] + n("n1e" + kk), n("f1%s%d" % (kk, z)), w, GEST)
+                vg(lambda y=y, c0=c0, c1=c1, o=o, w=w: V.tensor_tensor(d1[:, y, c0:c1], win.indirect(nl[:, 64 + o:64 + o + w // 16]), f1[:, y, c0:c1], A.subtract),
+                   ["xa", "xb"] + n("n1o" + kk, "f1%s%d" % (kk, z)), n("d1%s%d" % (kk, z)), w)
+                if z == NP1 - 1 or y == 1:
+                    c0 = 0 if y == 0 else c0
+                    dk = n(*["d1%s%d" % (kk, x) for x in (range(NP1) if y == 0 else [z])])
+                    s(lambda y=y, c0=c0, c1=c1: S.activation(d1[:, y, c0:c1], d1[:, y, c0:c1], AF.Abs), dk, dk, c1 - c0)
+        wsum(ps[2][:, 0:64], [("wz", lambda r: d1[:, :, r::16])], "ps2", n(*["d1%s%d" % (x, z) for x in "cr" for z in range(NP1)]), 64)
         m1 = tb("m1")
         index(tb("iv1"), ps[2][:, 0:64], "ps2", m1[:], "m1", 64)
         tolist(nl[:, 128:144], m1[:, 0:2, :, 0::2], 1, "m1", "n2ec", 16)
@@ -282,19 +307,27 @@ def build(g, core, T, topo):
         tolist(nl[:, 160:176], m1[:, 0:2, :, 1::2], 1, "m1", "n2oc", 16)
         tolist(nl[:, 176:192], m1[:, 2:4, 1, :], 1, "m1", "n2or", 16)
         f2, d2 = tb("f2"), tb("d2")
-        s(lambda: S.activation(f2[:], win.indirect(nl[:, 128:160]), AF.Copy), ["xa", "xb"] + n("n2ec", "n2er"), n("f2"), 512, GEST)
-        vg(lambda: V.tensor_tensor(d2[:], win.indirect(nl[:, 160:192]), f2[:], A.subtract), ["xa", "xb"] + n("n2oc", "n2or", "f2"), n("d2"), 512)
-        s(lambda: S.activation(d2[:], d2[:], AF.Abs), n("d2"), n("d2"), 512)
-        wsum(ps[0][:, 0:32], [("wz", lambda r: d2[:, r::16])], "ps0", n("d2"), 32, lambda r: 2 * (r % 8) + r // 8)
+        d2k = []
+        for y in range(NP2):
+            w, yk = 512 // NP2, ["c"] if NP2 == 2 and y == 0 else ["r"] if NP2 == 2 else ["c", "r"]
+            c0, c1, o = y * w, y * w + w, 128 + y * w // 16
+            s(lambda c0=c0, c1=c1, o=o, w=w: S.activation(f2[:, c0:c1], win.indirect(nl[:, o:o + w // 16]), AF.Copy),
+              ["xa", "xb"] + n(*["n2e" + x for x in yk]), n("f2%d" % y), w, GEST)
+            vg(lambda c0=c0, c1=c1, o=o, w=w: V.tensor_tensor(d2[:, c0:c1], win.indirect(nl[:, 32 + o:32 + o + w // 16]), f2[:, c0:c1], A.subtract),
+               ["xa", "xb"] + n("f2%d" % y, *["n2o" + x for x in yk]), n("d2%d" % y), w)
+            s(lambda c0=c0, c1=c1: S.activation(d2[:, c0:c1], d2[:, c0:c1], AF.Abs), n("d2%d" % y), n("d2%d" % y), w)
+            d2k += n("d2%d" % y)
+        wsum(ps[0][:, 0:32], [("wz", lambda r: d2[:, r::16])], "ps0", d2k, 32, lambda r: 2 * (r % 8) + r // 8)
         iv2 = tb("iv2")
         index(iv2, ps[0][:, 0:32], "ps0", iv2[:, 4, :], "m2", 32)
         tolist(nl[:, 200:216], iv2[:, 4, 16:32], 2, "m2", "n3r", 16)
         tolist(nl[:, 192:200], iv2[:, 4, 0:16:2], 2, "m2", "n3e", 8)
         tolist(nl[:, 216:224], iv2[:, 4, 1:16:2], 2, "m2", "n3o", 8)
         f3, d3c, d3r, a3 = tb("f3"), tb("d3c"), tb("d3r"), tb("a3")
-        s(lambda: S.activation(f3[:], win.indirect(nl[:, 192:216]), AF.Copy), ["xa", "xb"] + n("n3e", "n3r"), n("f3"), 384, GEST)
-        vg(lambda: V.tensor_tensor(d3c[:], win.indirect(nl[:, 216:224]), f3[:, 0:128], A.subtract), ["xa", "xb"] + n("n3o", "f3"), n("d3c"), 128)
-        v(lambda: V.tensor_tensor(d3r[:], f3[:, 128:384:2], f3[:, 129:384:2], A.subtract), n("f3"), n("d3r"), 128, 2)
+        s(lambda: S.activation(f3[:, 0:128], win.indirect(nl[:, 192:200]), AF.Copy), ["xa", "xb"] + n("n3e"), n("f3c"), 128, GEST)
+        s(lambda: S.activation(f3[:, 128:384], win.indirect(nl[:, 200:216]), AF.Copy), ["xa", "xb"] + n("n3r"), n("f3r"), 256, GEST)
+        vg(lambda: V.tensor_tensor(d3c[:], win.indirect(nl[:, 216:224]), f3[:, 0:128], A.subtract), ["xa", "xb"] + n("n3o", "f3c"), n("d3c"), 128)
+        v(lambda: V.tensor_tensor(d3r[:], f3[:, 128:384:2], f3[:, 129:384:2], A.subtract), n("f3r"), n("d3r"), 128, 2)
         for y in range(2):
             s(lambda y=y: S.activation(a3[:, 0, :, y, :], d3c[:, y:128:2], AF.Abs), n("d3c"), n("a3c%d" % y), 64)
         s(lambda: S.activation(a3[:, 1, :, :, :], d3r[:], AF.Abs), n("d3r"), n("a3r"), 128)
@@ -332,7 +365,8 @@ def build(g, core, T, topo):
         v(lambda: V.tensor_tensor(sf[:, 16:24], qrt, sf[:, 40:48], A.mult), n("cw") + ["qr%d%d" % (t, h), "sfz" + H], n("mwc"), 8)
         v(lambda: V.tensor_tensor(sf[:, 24:32], qrt, sf[:, 40:48], A.is_gt), n("cw") + ["qr%d%d" % (t, h), "sfz" + H], n("mwr"), 8)
         ly = tb("ly")
-        s(lambda: S.activation(ly[:], sf[:, 16:40].indirect(T.exl[:, 16:40]), AF.Copy), ["exy0", "exy1", "sfz" + H] + n("mwc", "mwr"), n("ly"), 384, GEST)
+        s(lambda: S.activation(ly[:, 0:256], sf[:, 16:40].indirect(T.exl[:, 16:32]), AF.Copy), ["exy0", "sfz" + H] + n("mwc", "mwr"), n("lyc"), 256, GEST)
+        vg(lambda: V.tensor_copy(ly[:, 256:384], sf[:, 16:40].indirect(T.exl[:, 32:40])), ["exy1", "sfz" + H] + n("mwc", "mwr"), n("lyr"), 128)
         bf, xm, dl, b2 = tb("bf"), tb("xm"), tb("dl"), tb("b2")
         v(lambda: V.tensor_copy(bf[:, 0:128], lb[:, t, :]), LB, n("bf"), 128)
         bp = ps[0][:, 256:384]
@@ -342,7 +376,7 @@ def build(g, core, T, topo):
         pe([lambda k=k: P.matmul(ps[3][:, 0:129], lt[:, 128 * k:128 * k + 128], T.ch[:, k, 0:129], False, k == 1) for k in range(2)],
            CH + n("lt"), n("ps3"), 129, 4)
         pe([lambda k=k: P.matmul(ps[1][:, 0:128], ly[:, 128 * k:128 * k + 128], T.sel[:, k, :], k == 0, k == 2) for k in range(3)],
-           ["sel0", "sel1", "sel2"] + n("ly"), n("ps1"), 128)
+           ["sel0", "sel1", "sel2"] + n("lyc", "lyr"), n("ps1"), 128)
         v(lambda: V.tensor_scalar(xm[:], ps[1][:, 0:128], 1.0, ps[3][:, 128:129], A.is_equal, A.mult), [], n("ps1", "ps3", "xm"), 128)
         v(lambda: V.tensor_tensor(dl[:], ps[3][:, 0:128], xm[:], A.mult), n("xm"), n("ps3", "dl"), 128)
         if t < ROUNDS - 1:
@@ -409,7 +443,7 @@ def schedule(ops):
         o = ops[i]
         prio[i] = o["c"] + o["lat"] + max([0.03 + prio[j] for j in succ[i]] or [0.0])
     for i, o in enumerate(ops):
-        prio[i] = o.get("first", prio[i] - BIAS * o["b"] + TUNE.get(o["k"], 0.0))
+        prio[i] = o.get("first", prio[i] - BIAS * o["b"] + OFFS * (o["b"] % 2) + TUNE.get(o["k"], 0.0))
     left = [len(o["d"]) for o in ops]
     ready = [0.0] * nops
     queues = ("V", "S", "P", "G", "Y", "N")
@@ -429,6 +463,15 @@ def schedule(ops):
         if bq is None:
             return order
         i = max((j for j in cand[bq] if ready[j] <= best), key=lambda j: prio[j])
+        late = [j for j in cand[bq] if prio[j] > prio[i] and best < ready[j] < best + AHEAD * ops[i]["c"]]
+        if late and bq != "N":
+            j = min(late, key=lambda j: ready[j])
+            fits = [k for k in cand[bq] if ready[k] + ops[k]["c"] <= ready[j] and ready[k] <= best]
+            if fits:
+                i = max(fits, key=lambda k: prio[k])
+            else:
+                free[bq] = ready[j]
+                continue
         o = ops[i]
         cand[bq].remove(i)
         order.append(i)
@@ -439,7 +482,7 @@ def schedule(ops):
         o["t"] = (best, e)
         for j in succ[i]:
             left[j] -= 1
-            ready[j] = max(ready[j], e + (0.03 if ops[j]["q"] == bq else 0.08))
+            ready[j] = max(ready[j], e + (EST["wl"] if ops[j]["q"] == bq else EST["wc"]))
             if not left[j]:
                 cand[ops[j]["q"]].add(j)
 

@@ -14,7 +14,8 @@ SCRATCH = {
     "j16": ("sbuf", [128, 1], F32), "j8": ("sbuf", [128, 3], F32),
     "ones": ("sbuf", [128, 128], F32), "ms1": ("sbuf", [128, 128], F32), "bl": ("sbuf", [128, 128], F32),
     "cm": ("sbuf", [128, 2, 16], F32), "thp": ("sbuf", [128, 2], I32), "thq": ("sbuf", [128, 2], F32),
-    "dth": ("sbuf", [128, 2, 128], BF), "onb": ("sbuf", [128, 8], BF),
+    "dth": ("sbuf", [128, 2, 128], BF), "onb": ("sbuf", [128, 64], BF),
+    "bias": ("sbuf", [128, 256], BF), "j7": ("sbuf", [128, 1], F32),
     "idn": ("sbuf", [128, 128], F32), "nid": ("sbuf", [128, 128], F32), "idb": ("sbuf", [128, 128], BF), "nib": ("sbuf", [128, 128], BF),
     "wz": ("sbuf", [128, 144], BF), "uz": ("sbuf", [128, 144], BF), "wb": ("sbuf", [128, 128], BF),
     "w2z": ("sbuf", [128, 144], BF), "nwz": ("sbuf", [128, 144], BF),
@@ -38,7 +39,7 @@ for _h in range(2):
             ("ivc", [128, 4, 64], I32), ("ivr", [128, 4, 64], I32), ("iv1", [128, 4, 64], I32),
             ("iv2", [128, 5, 32], I32), ("iv3", [128, 5, 16], I32),
             ("mc", [128, 32, 2], I32), ("mr", [128, 4, 2, 8], I32), ("m1", [128, 4, 2, 8], I32),
-            ("si", [128, 64], I32), ("sf", [128, 48], F32),
+            ("si", [128, 64], I32), ("sf", [128, 72], F32),
             ("oh", [128, 9], F32), ("cu", [128, 9], F32),
             ("lt", [128, 256], F32), ("ltt", [128, 256], F32), ("ly", [128, 384], BF),
             ("bf", [128, 132], F32), ("xm", [128, 128], F32), ("dl", [128, 128], F32), ("b2", [128, 128], F32),
@@ -54,15 +55,16 @@ ABS0 = "SSSS"
 DGATH = "V"
 L0PE = True
 NP1, NP2 = 2, 2
+M12, M4 = 1.5 * 2.0 ** 35, 1.5 * 2.0 ** 27
 ABS1 = "SS"
 GEST = 1.5
-BIAS = 8.0
-OFFS = 6.0
-AHEAD = 0.15
+BIAS = 3.0
+OFFS = 1.5
+AHEAD = 0.35
 TUNE = {}
 
 
-EST = {"cyc": 0.001, "g": 1.7, "pe": 0.0007, "v0": 0.02, "s0": 0.06, "p0": 0.03, "wl": 0.08, "wc": 0.16}
+EST = {"cyc": 0.001, "g": 1.35, "pe": 0.0005, "v0": 0.02, "s0": 0.06, "p0": 0.03, "wl": 0.12, "wc": 0.1}
 
 
 def estimate(m, e):
@@ -90,7 +92,7 @@ def build(g, core, T, topo):
     V, S, P = g.vector, g.scalar, g.tensor
     ops = []
     cur = [0, None]
-    lastw, readers = {}, {}
+    lastw, readers, banks = {}, {}, {}
 
     def op(q, fns, r=(), w=(), cost=0.1, grp=None, sem=None, lat=0.0):
         deps = set()
@@ -102,6 +104,16 @@ def build(g, core, T, topo):
                 deps.update(lastw[k])
             deps.update(readers.get(k, ()))
         i = len(ops)
+        for k in w:
+            if k[:2] == "ps":
+                b = banks.setdefault(k, {"q": None, "cur": [], "prev": []})
+                if b["q"] != q:
+                    b["q"], b["prev"], b["cur"] = q, b["cur"], []
+                deps.update(b["prev"])
+                if q == "P":
+                    deps.update(b["cur"][-1:])
+                b["cur"].append(i)
+        w = [k for k in w if k[:2] != "ps"]
         for k in w:
             lastw[k] = [i]
             readers[k] = []
@@ -146,7 +158,7 @@ def build(g, core, T, topo):
     first(3.0, "Y", T.wti[:], T.wt[:], ["wti"], "lw")
     for c in range(8):
         first(7.0, "Y", T.raw[:, 1, beta(c), :], T.bn[c::8, 128:256], ["raw1_%d" % c], "lr1")
-    first(9.0, "Y", T.xx[:, 4096:4096 + 3920], T.xf[:, 0:3920], ["xb"], "lxb")
+    first(9.0, "Y", T.xx[:, 4096:8192], T.xf[:], ["xb"], "lxb")
     first(9.0, "Y", T.thi[:], T.th[:], ["thi"], "lth")
     for c in range(16):
         first(11.0, "Y", T.raw[:, 2 + c // 8, beta(c), :], T.cn[c::16, :], ["raw%d_%d" % (2 + c // 8, c % 8)], "lr%d" % (2 + c // 8))
@@ -190,13 +202,17 @@ def build(g, core, T, topo):
     v(lambda: V.tensor_scalar(T.exl[:, 16:32], T.cm[:, 0, :], T.j8[:, 1:2], 16.0, A.mult, A.add), ["cm0", "j8b"], ["exy0"], 16)
     v(lambda: V.tensor_scalar(T.exl[:, 32:40], T.bl[:, 0:128:16], T.j8[:, 0:1], 16.0, A.mult, A.add), ["bl", "j8a"], ["exy1"], 8)
     for h in range(2):
-        v(lambda h=h: V.memset(T["sf%d" % h][:], 0.0), [], ["sfz%d" % h], 48)
+        v(lambda h=h: V.memset(T["sf%d" % h][:], 0.0), [], ["sfz%d" % h], 72)
     v(lambda: V.tensor_scalar(T.thp[:, 0:1], T.thi[:], 4080, None, A.bitwise_and), ["thi"], ["thp0"], 1)
     v(lambda: V.tensor_scalar(T.thp[:, 1:2], T.thi[:], 15, None, A.bitwise_and), ["thi"], ["thp1"], 1)
     v(lambda: V.tensor_scalar(T.thq[:], T.thp[:], -1.0, None, A.mult), ["thp0", "thp1"], ["thq"], 2)
     for k in range(2):
         v(lambda k=k: V.tensor_scalar(T.dth[:, k, :], T.idn[:], T.thq[:, k:k + 1], None, A.mult), ["idn", "thq"], ["dth%d" % k], 128)
-    v(lambda: V.memset(T.onb[:], 1.0), [], ["onb"], 8)
+    v(lambda: V.memset(T.onb[:], 1.0), [], ["onb"], 64)
+    v(lambda: V.memset(T.bias[:, 0:128], -16.0), [], ["bias"], 128)
+    v(lambda: V.memset(T.bias[0:1, 0:128], -15.5), [], ["bias"], 128)
+    v(lambda: V.memset(T.bias[:, 128:256], -0.05859375), [], ["bias7"], 128)
+    v(lambda: V.tensor_scalar(T.j7[:], T.j16[:], -1.0, 7.5, A.mult, A.add), ["j16"], ["j7"], 1)
     v(lambda: V.memset(T.rs[:], 1.0), [], ["rs"], 9)
     v(lambda: V.memset(T.oh0[:], 0.0), [], ["oh0", "ohc0"], 9)
     v(lambda: V.memset(T.bf0[:, 128:132], 0.0), [], ["bfz0"], 4)
@@ -221,7 +237,7 @@ def build(g, core, T, topo):
         ps = [T["ps%d%d" % (h, b)] for b in range(4)]
         ne = len(engs)
         win0 = T.xx[:, 0:4096]
-        win = T.xx[:, 0:8192]
+        wins, wk = [T.xx[:, 0:8192]] * 4, [["xa", "xb"]] * 4
         lb = tb("lb")
         nl = tb("nl")
         if t == 0:
@@ -253,26 +269,24 @@ def build(g, core, T, topo):
             s(lambda reg=reg, b=b: S.activation(z0[:, reg, :], ps[b][:, 0:512], AF.Abs), [], n("ps%d" % b, "z0_%d" % reg), 512)
 
         def wsum(out, parts, bank, keys, per_r, to=lambda r: r):
+            pe([lambda: P.matmul(out, T.bias[:, 0:128], T.onb[:, 0:per_r], True, False)], ["bias", "onb"], n(bank), per_r)
             fns = []
-            tot = 16 * len(parts)
-            k = 0
             for lz, f in parts:
                 for r in range(16):
-                    fns.append(lambda lz=lz, f=f, r=r, k=k: P.matmul(out, T[lz][:, 15 - to(r):143 - to(r)], f(r), k == 0, k == tot - 1))
-                    k += 1
+                    fns.append(lambda lz=lz, f=f, r=r: P.matmul(out, T[lz][:, 15 - to(r):143 - to(r)], f(r), False, r == 15))
             pe(fns, [p[0] for p in parts] + keys, n(bank), per_r)
 
         def index(iv, src, bank, m, mkey, nn):
             i = mkey
             tmp = ps[int(bank[2])][:, 384:384 + nn]
-            v(lambda: V.tensor_copy(iv[:, 0, :], src), [], n(bank, i + "0"), nn)
-            v(lambda: V.tensor_scalar(iv[:, 1, :], iv[:, 0, :], 4095, None, A.bitwise_and), n(i + "0"), n(i + "1"), nn)
-            v(lambda: V.tensor_scalar(tmp, iv[:, 1, :], 1184, None, A.add), n(i + "1"), n(bank), nn)
-            v(lambda: V.tensor_tensor(iv[:, 3, :], iv[:, 1, :], tmp, A.mult), n(i + "1"), n(bank, i + "3"), nn)
+            v(lambda: V.tensor_scalar(iv[:, 0, :], src, M12, M12, A.add, A.subtract), [], n(bank, i + "0"), nn)
+            v(lambda: V.tensor_scalar(tmp, src, 2639.5, None, A.add), [], n(bank, "t" + bank), nn)
+            v(lambda: V.tensor_tensor(iv[:, 1, :], tmp, iv[:, 0, :], A.subtract), n(i + "0", "t" + bank), n(bank, i + "1"), nn)
+            v(lambda: V.tensor_tensor(iv[:, 3, :], iv[:, 1, :], iv[:, 1, :], A.mult), n(i + "1"), n(i + "3"), nn, 2)
             v(lambda: V.tensor_scalar(m, iv[:, 3, :], 5, 4095, A.arith_shift_right, A.bitwise_and), n(i + "3"), n(i), nn)
 
         def tolist(out, in_, k, mkey, w, nn):
-            v(lambda: V.tensor_scalar(out, in_, KAP[k], None, A.add), n(mkey), n(w), nn)
+            v(lambda: V.tensor_scalar(out, in_, (KAP[k] - 10952) % 4096, None, A.add), n(mkey), n(w), nn)
 
         for a, b, kk in ((0, 2, "c"), (2, 4, "r")):
             bank = "ps0" if kk == "c" else "ps1"
@@ -291,10 +305,10 @@ def build(g, core, T, topo):
             for z in range(NP1):
                 w = 512 // NP1
                 c0, c1, o = z * w, z * w + w, 32 * y + z * w // 16
-                s(lambda y=y, c0=c0, c1=c1, o=o, w=w: S.activation(f1[:, y, c0:c1], win.indirect(nl[:, o:o + w // 16]), AF.Copy),
-                  ["xa", "xb"] + n("n1e" + kk), n("f1%s%d" % (kk, z)), w, GEST)
-                vg(lambda y=y, c0=c0, c1=c1, o=o, w=w: V.tensor_tensor(d1[:, y, c0:c1], win.indirect(nl[:, 64 + o:64 + o + w // 16]), f1[:, y, c0:c1], A.subtract),
-                   ["xa", "xb"] + n("n1o" + kk, "f1%s%d" % (kk, z)), n("d1%s%d" % (kk, z)), w)
+                s(lambda y=y, c0=c0, c1=c1, o=o, w=w: S.activation(f1[:, y, c0:c1], wins[0].indirect(nl[:, o:o + w // 16]), AF.Copy),
+                  wk[0] + n("n1e" + kk), n("f1%s%d" % (kk, z)), w, GEST)
+                vg(lambda y=y, c0=c0, c1=c1, o=o, w=w: V.tensor_tensor(d1[:, y, c0:c1], wins[0].indirect(nl[:, 64 + o:64 + o + w // 16]), f1[:, y, c0:c1], A.subtract),
+                   wk[0] + n("n1o" + kk, "f1%s%d" % (kk, z)), n("d1%s%d" % (kk, z)), w)
                 if z == NP1 - 1 or y == 1:
                     c0 = 0 if y == 0 else c0
                     dk = n(*["d1%s%d" % (kk, x) for x in (range(NP1) if y == 0 else [z])])
@@ -311,10 +325,10 @@ def build(g, core, T, topo):
         for y in range(NP2):
             w, yk = 512 // NP2, ["c"] if NP2 == 2 and y == 0 else ["r"] if NP2 == 2 else ["c", "r"]
             c0, c1, o = y * w, y * w + w, 128 + y * w // 16
-            s(lambda c0=c0, c1=c1, o=o, w=w: S.activation(f2[:, c0:c1], win.indirect(nl[:, o:o + w // 16]), AF.Copy),
-              ["xa", "xb"] + n(*["n2e" + x for x in yk]), n("f2%d" % y), w, GEST)
-            vg(lambda c0=c0, c1=c1, o=o, w=w: V.tensor_tensor(d2[:, c0:c1], win.indirect(nl[:, 32 + o:32 + o + w // 16]), f2[:, c0:c1], A.subtract),
-               ["xa", "xb"] + n("f2%d" % y, *["n2o" + x for x in yk]), n("d2%d" % y), w)
+            s(lambda c0=c0, c1=c1, o=o, w=w: S.activation(f2[:, c0:c1], wins[1].indirect(nl[:, o:o + w // 16]), AF.Copy),
+              wk[1] + n(*["n2e" + x for x in yk]), n("f2%d" % y), w, GEST)
+            vg(lambda c0=c0, c1=c1, o=o, w=w: V.tensor_tensor(d2[:, c0:c1], wins[1].indirect(nl[:, 32 + o:32 + o + w // 16]), f2[:, c0:c1], A.subtract),
+               wk[1] + n("f2%d" % y, *["n2o" + x for x in yk]), n("d2%d" % y), w)
             s(lambda c0=c0, c1=c1: S.activation(d2[:, c0:c1], d2[:, c0:c1], AF.Abs), n("d2%d" % y), n("d2%d" % y), w)
             d2k += n("d2%d" % y)
         wsum(ps[0][:, 0:32], [("wz", lambda r: d2[:, r::16])], "ps0", d2k, 32, lambda r: 2 * (r % 8) + r // 8)
@@ -324,9 +338,9 @@ def build(g, core, T, topo):
         tolist(nl[:, 192:200], iv2[:, 4, 0:16:2], 2, "m2", "n3e", 8)
         tolist(nl[:, 216:224], iv2[:, 4, 1:16:2], 2, "m2", "n3o", 8)
         f3, d3c, d3r, a3 = tb("f3"), tb("d3c"), tb("d3r"), tb("a3")
-        s(lambda: S.activation(f3[:, 0:128], win.indirect(nl[:, 192:200]), AF.Copy), ["xa", "xb"] + n("n3e"), n("f3c"), 128, GEST)
-        s(lambda: S.activation(f3[:, 128:384], win.indirect(nl[:, 200:216]), AF.Copy), ["xa", "xb"] + n("n3r"), n("f3r"), 256, GEST)
-        vg(lambda: V.tensor_tensor(d3c[:], win.indirect(nl[:, 216:224]), f3[:, 0:128], A.subtract), ["xa", "xb"] + n("n3o", "f3c"), n("d3c"), 128)
+        s(lambda: S.activation(f3[:, 0:128], wins[2].indirect(nl[:, 192:200]), AF.Copy), wk[2] + n("n3e"), n("f3c"), 128, GEST)
+        s(lambda: S.activation(f3[:, 128:384], wins[2].indirect(nl[:, 200:216]), AF.Copy), wk[2] + n("n3r"), n("f3r"), 256, GEST)
+        vg(lambda: V.tensor_tensor(d3c[:], wins[2].indirect(nl[:, 216:224]), f3[:, 0:128], A.subtract), wk[2] + n("n3o", "f3c"), n("d3c"), 128)
         v(lambda: V.tensor_tensor(d3r[:], f3[:, 128:384:2], f3[:, 129:384:2], A.subtract), n("f3r"), n("d3r"), 128, 2)
         for y in range(2):
             s(lambda y=y: S.activation(a3[:, 0, :, y, :], d3c[:, y:128:2], AF.Abs), n("d3c"), n("a3c%d" % y), 64)
@@ -336,14 +350,15 @@ def build(g, core, T, topo):
         index(iv3, ps[1][:, 0:16], "ps1", iv3[:, 4, :], "m3", 16)
         tolist(nl[:, 224:240], iv3[:, 4, :], 3, "m3", "n4", 16)
         q3 = tb("q3")
-        s(lambda: S.activation(q3[:, 0, :], win.indirect(nl[:, 224:232]), AF.Copy), ["xa", "xb"] + n("n4"), n("q30"), 128, GEST)
-        vg(lambda: V.tensor_tensor(q3[:, 1, :], win.indirect(nl[:, 232:240]), q3[:, 0, :], A.subtract), ["xa", "xb"] + n("n4", "q30"), n("q31"), 128)
+        s(lambda: S.activation(q3[:, 0, :], wins[3].indirect(nl[:, 224:232]), AF.Copy), wk[3] + n("n4"), n("q30"), 128, GEST)
+        vg(lambda: V.tensor_tensor(q3[:, 1, :], wins[3].indirect(nl[:, 232:240]), q3[:, 0, :], A.subtract), wk[3] + n("n4", "q30"), n("q31"), 128)
         s(lambda: S.activation(q3[:, 2, :], q3[:, 1, :], AF.Abs), n("q31"), n("q32"), 128)
         si, sf, oh, cu = tb("si"), tb("sf"), tb("oh"), tb("cu")
-        pe([lambda: P.matmul(ps[0][:, 0:8], T.wb[:], q3[:, 0, 0:8], True, True)], ["wb"] + n("q30"), n("ps0"), 8)
-        v(lambda: V.tensor_copy(si[:, 0:8], ps[0][:, 0:8]), [], n("ps0", "di"), 8)
-        v(lambda: V.tensor_scalar(si[:, 16:24], si[:, 0:8], 15, None, A.bitwise_and), n("di"), n("da"), 8)
-        v(lambda: V.tensor_scalar(oh[:, 1:9], si[:, 16:24], T.j16[:, 0:1], None, A.is_equal), ["j16", "oh" + H] + n("da"), n("oh"), 8)
+        pe([lambda: P.matmul(ps[0][:, 0:8], T.bias[:, 128:256], T.onb[:, 0:8], True, False)], ["bias7", "onb"], n("ps0"), 8)
+        pe([lambda: P.matmul(ps[0][:, 0:8], T.wb[:], q3[:, 0, 0:8], False, True)], ["wb"] + n("q30"), n("ps0"), 8)
+        v(lambda: V.tensor_scalar(si[:, 0:8], ps[0][:, 0:8], M4, M4, A.add, A.subtract), [], n("ps0", "di"), 8)
+        v(lambda: V.tensor_scalar(si[:, 16:24], ps[0][:, 0:8], T.j7[:, 0:1], None, A.add), ["j7"], n("ps0", "da"), 8)
+        v(lambda: V.tensor_tensor(oh[:, 1:9], si[:, 16:24], si[:, 0:8], A.is_equal), ["oh" + H] + n("da", "di"), n("oh"), 8)
         v(lambda: V.tensor_tensor_scan(cu[:], T.rs[:], oh[:], 0.0, A.mult, A.max), ["rs", "oh" + H, "ohc" + H] + n("oh"), n("cu"), 9)
         if h == 0:
             s(lambda: S.activation(T.oh1[:, 0:1], T.cu0[:, 8:9], AF.Copy), n("cu"), ["ohc1"], 1)
@@ -355,15 +370,17 @@ def build(g, core, T, topo):
             r = house(kap)
             fns.append(lambda kap=kap, r=r: P.matmul(ps[2][:, 0:24], T.uz[:, 15 - r:143 - r], q3[:, :, 8 * kap:8 * kap + 8], kap == 0, False))
         for k in range(2):
-            fns.append(lambda k=k: P.matmul(ps[2][:, 16:24], T.dth[:, k, :], T.onb[:], False, k == 1))
+            fns.append(lambda k=k: P.matmul(ps[2][:, 16:24], T.dth[:, k, :], T.onb[:, 0:8], False, k == 1))
         pe(fns, ["uz", "dth0", "dth1", "onb"] + n("q30", "q31", "q32"), n("ps2"), 24)
         v(lambda: V.tensor_copy(si[:, 32:40], ps[2][:, 0:8]), [], n("ps2", "qi"), 8)
         v(lambda: V.tensor_scalar(si[:, 56:64], si[:, 32:40], 15, None, A.bitwise_and), n("qi"), n("qa"), 8)
-        v(lambda: V.tensor_scalar(sf[:, 40:48], ps[2][:, 8:16], 0.0, None, A.is_ge), ["sfz" + H], n("ps2", "cw"), 8)
+        for y, cmp in ((0, A.is_ge), (1, A.is_lt)):
+            v(lambda y=y, cmp=cmp: V.tensor_scalar(sf[:, 40 + 8 * y:48 + 8 * y], ps[2][:, 8:16], 0.0, 9000.0, cmp, A.mult), ["sfz" + H], n("ps2", "cw%d" % y), 8)
+            v(lambda y=y: V.tensor_tensor(sf[:, 56 + 8 * y:64 + 8 * y], ps[2][:, 16:24], sf[:, 40 + 8 * y:48 + 8 * y], A.min), n("cw%d" % y) + ["sfz" + H], n("ps2", "dm%d" % y), 8)
+        for y in range(2):
+            v(lambda y=y: V.tensor_tensor(sf[:, 16 + 8 * y:24 + 8 * y], sf[:, 56 + 8 * y:64 + 8 * y], si[:, 56:64], A.is_gt), n("qa", "dm%d" % y) + ["sfz" + H], n("mw" + "cr"[y]), 8)
         qrt = T.qr[:, t, 8 * h:8 * h + 8]
-        v(lambda: V.tensor_tensor(qrt, ps[2][:, 16:24], si[:, 56:64], A.is_gt), n("qa"), n("ps2") + ["qr%d%d" % (t, h)], 8)
-        v(lambda: V.tensor_tensor(sf[:, 16:24], qrt, sf[:, 40:48], A.mult), n("cw") + ["qr%d%d" % (t, h), "sfz" + H], n("mwc"), 8)
-        v(lambda: V.tensor_tensor(sf[:, 24:32], qrt, sf[:, 40:48], A.is_gt), n("cw") + ["qr%d%d" % (t, h), "sfz" + H], n("mwr"), 8)
+        v(lambda: V.tensor_tensor(qrt, sf[:, 16:24], sf[:, 24:32], A.add), n("mwc", "mwr"), ["qr%d%d" % (t, h)], 8)
         ly = tb("ly")
         s(lambda: S.activation(ly[:, 0:256], sf[:, 16:40].indirect(T.exl[:, 16:32]), AF.Copy), ["exy0", "sfz" + H] + n("mwc", "mwr"), n("lyc"), 256, GEST)
         vg(lambda: V.tensor_copy(ly[:, 256:384], sf[:, 16:40].indirect(T.exl[:, 32:40])), ["exy1", "sfz" + H] + n("mwc", "mwr"), n("lyr"), 128)

from concourse.bass import DstId, RemoteDMATransfer
from concourse.mybir import dt, AluOpType, ActivationFunctionType

A = AluOpType
AF = ActivationFunctionType
ROUNDS = 4
KAP = (101, 1303, 2717, 3911)
BF, F32, I32, U16 = "bfloat16", "float32", "int32", "uint16"

SCRATCH = {
    "xx": ("sbuf", [128, 8192], BF),
    "wti": ("sbuf", [128, 1], I32), "thi": ("sbuf", [128, 1], I32), "wf": ("sbuf", [128, 1], F32),
    "pid": ("sbuf", [128, 3], I32),
    "j16": ("sbuf", [128, 1], F32), "j8": ("sbuf", [128, 3], F32),
    "ones": ("sbuf", [128, 128], F32), "ms1": ("sbuf", [128, 128], F32), "bl": ("sbuf", [128, 128], F32),
    "cm": ("sbuf", [128, 2, 16], F32), "thp": ("sbuf", [128, 2], I32), "thq": ("sbuf", [128, 2], F32),
    "dth": ("sbuf", [128, 2, 128], BF), "onb": ("sbuf", [128, 64], BF),
    "bias": ("sbuf", [128, 256], BF), "j7": ("sbuf", [128, 1], F32),
    "idn": ("sbuf", [128, 128], F32), "nid": ("sbuf", [128, 128], F32), "idb": ("sbuf", [128, 128], BF), "nib": ("sbuf", [128, 128], BF),
    "wz": ("sbuf", [128, 144], BF), "uz": ("sbuf", [128, 144], BF), "wb": ("sbuf", [128, 128], BF),
    "w2z": ("sbuf", [128, 144], BF), "nwz": ("sbuf", [128, 144], BF),
    "pf": ("sbuf", [128, 128], F32), "cf": ("sbuf", [128, 128], F32),
    "sel": ("sbuf", [128, 3, 128], BF), "exl": ("sbuf", [128, 40], U16),
    "rs": ("sbuf", [128, 9], F32),
    "raw": ("sbuf", [128, 4, 8, 16], I32),
    "ch": ("sbuf", [128, 2, 132], F32),
    "yqs": ("sbuf", [128, 16], F32),
    "qr": ("sbuf", [128, 4, 16], BF),
    "roc": ("sbuf", [128, 2, 8, 16], F32),
}
for _h in range(2):
    for _n, _s, _d in (
            ("f0", [128, 2, 512], BF), ("d0", [128, 4, 512], BF), ("z0", [128, 4, 512], BF),
            ("f1", [128, 2, 512], BF), ("d1", [128, 2, 512], BF), ("z1", [128, 2, 512], BF),
            ("f2", [128, 512], BF), ("d2", [128, 512], BF),
            ("f3", [128, 384], BF), ("d3c", [128, 128], BF), ("d3r", [128, 128], BF), ("a3", [128, 2, 2, 2, 32], BF),
            ("q3", [128, 3, 128], BF),
            ("nl", [128, 240], U16),
            ("ivc", [128, 4, 64], I32), ("ivr", [128, 4, 64], I32), ("iv1", [128, 4, 64], I32),
            ("iv2", [128, 5, 32], I32), ("iv3", [128, 5, 16], I32),
            ("mc", [128, 32, 2], I32), ("mr", [128, 4, 2, 8], I32), ("m1", [128, 4, 2, 8], I32),
            ("si", [128, 64], I32), ("sf", [128, 72], F32),
            ("oh", [128, 9], F32), ("cu", [128, 9], F32),
            ("lt", [128, 256], F32), ("ltt", [128, 256], F32), ("ly", [128, 384], BF),
            ("bf", [128, 132], F32), ("xm", [128, 128], F32), ("dl", [128, 128], F32), ("b2", [128, 128], F32),
            ("rob", [128, 8, 16], F32),
            ("lb", [128, 4, 128], U16), ("sn", [128, 3, 128], U16)):
        SCRATCH[_n + str(_h)] = ("sbuf", _s, _d)
    for _b in range(4):
        SCRATCH["ps%d%d" % (_h, _b)] = ("psum", [128, 512], F32)
SEMAPHORES = ["eV", "eS", "eP", "eG", "snd", "lxa", "lxb", "lw", "lth", "lr0", "lr1", "lr2", "lr3", "ost"]
SEMAPHORES += ["rc%d%d" % (_t, _h) for _t in range(1, ROUNDS) for _h in range(2)]

ABS0 = "SSSS"
DGATH = "V"
L0PE = True
NP1, NP2 = 2, 2
M12, M4 = 1.5 * 2.0 ** 35, 1.5 * 2.0 ** 27
ABS1 = "SS"
GEST = 1.5
BIAS = 3.0
OFFS = 1.5
AHEAD = 0.35
TUNE = {}


EST = {"cyc": 0.001, "g": 1.35, "pe": 0.0005, "v0": 0.02, "s0": 0.06, "p0": 0.03, "wl": 0.12, "wc": 0.1}


def estimate(m, e):
    kind, n = m
    if kind == "v":
        return e["cyc"] * n + e["v0"]
    if kind == "vg":
        return 0.05 + e["cyc"] * e["g"] * n
    if kind == "s":
        return e["cyc"] * n + e["s0"]
    if kind == "sg":
        return 0.065 + e["cyc"] * e["g"] * n
    if kind == "p":
        return e["pe"] * n + e["p0"]
    return n


def house(k):
    return (k & 7) << 1 | k >> 3


def build(g, core, T, topo):
    rank = T.rank_of(core)
    dst = T.cores[(rank + 1) % len(T.cores)]
    V, S, P = g.vector, g.scalar, g.tensor
    ops = []
    cur = [0, None]
    lastw, readers, banks = {}, {}, {}

    def op(q, fns, r=(), w=(), cost=0.1, grp=None, sem=None, lat=0.0):
        deps = set()
        for k in r:
            if k in lastw:
                deps.update(lastw[k])
        for k in w:
            if k in lastw:
                deps.update(lastw[k])
            deps.update(readers.get(k, ()))
        i = len(ops)
        for k in w:
            if k[:2] == "ps":
                b = banks.setdefault(k, {"q": None, "cur": [], "prev": []})
                if b["q"] != q:
                    b["q"], b["prev"], b["cur"] = q, b["cur"], []
                deps.update(b["prev"])
                if q == "P":
                    deps.update(b["cur"][-1:])
                b["cur"].append(i)
        w = [k for k in w if k[:2] != "ps"]
        for k in w:
            lastw[k] = [i]
            readers[k] = []
        for k in r:
            if k not in w:
                readers.setdefault(k, []).append(i)
        if cur[1] is not None:
            cur[1] += 1
        m = cost if isinstance(cost, tuple) else ("c", cost)
        ops.append({"b": cur[0], "k": (cur[0] % 2, cur[1]), "q": q, "f": fns, "d": sorted(deps), "m": m, "c": estimate(m, EST),
                    "grp": grp, "lat": lat, "sem": sem})
        return i

    def v(fn, r, w, n, per=1.0):
        return op("V", [fn], r, w, ("v", max(64, n * per)))

    def vg(fn, r, w, n):
        return op("V", [fn], r, w, ("vg", n))

    def s(fn, r, w, n, per=1.0):
        return op("S", [fn], r, w, ("sg" if per > 1.0 else "s", n))

    def pe(fns, r, w, n, per=1.0):
        return op("P", fns, r, w, ("p", len(fns) * max(64, n) * per))

    def gc(fn, r, w, n):
        return op("G", [fn], r, w, 0.15 + 0.002 * n)

    def load(q, out, in_, w, grp, r=(), lat=2.2):
        eng = {"Y": g.sync, "S": g.scalar}[q]
        return op(q, [lambda: eng.dma_start(out, in_)], r, w, 0.08, grp, lat=lat)

    def first(lat, *a):
        ops[load(*a, lat=lat)]["first"] = 1e6 - len(ops)

    def beta(c):
        return (c & 1) << 2 | (c & 6) >> 1

    first(5.5, "Y", T.xx[:, 0:4096], T.xf[:], ["xa"], "lxa")
    for c in range(8):
        first(3.0, "S", T.raw[:, 0, beta(c), :], T.bn[c::8, 0:128], ["raw0_%d" % c], "lr0")
    first(3.0, "Y", T.wti[:], T.wt[:], ["wti"], "lw")
    for c in range(8):
        first(7.0, "Y", T.raw[:, 1, beta(c), :], T.bn[c::8, 128:256], ["raw1_%d" % c], "lr1")
    first(9.0, "Y", T.xx[:, 4096:8192], T.xf[:], ["xb"], "lxb")
    first(9.0, "Y", T.thi[:], T.th[:], ["thi"], "lth")
    for c in range(16):
        first(11.0, "Y", T.raw[:, 2 + c // 8, beta(c), :], T.cn[c::16, :], ["raw%d_%d" % (2 + c // 8, c % 8)], "lr%d" % (2 + c // 8))

    gc(lambda: g.iota(T.pid[:, 0:1], [[0, 1]], 0, 1), [], ["pid0"], 1)
    v(lambda: V.memset(T.ones[:], 1.0), [], ["ones"], 128)
    gc(lambda: g.affine_select(T.ms1[:], T.ones[:], [[-16, 8], [0, 16]], A.is_ge, 0.0, 0, 1), ["ones"], ["ms1b"], 128)
    gc(lambda: g.affine_select(T.bl[:], T.ms1[:], [[16, 8], [0, 16]], A.is_ge, 0.0, 15, -1), ["ms1b"], ["bl"], 128)
    gc(lambda: g.affine_select(T.cm[:, 1, :], T.ones[:, 0:16], [[-8, 2], [-16, 8]], A.is_ge, 0.0, 0, 1), ["ones"], ["cm1"], 16)
    gc(lambda: g.affine_select(T.cm[:, 0, :], T.cm[:, 1, :], [[8, 2], [16, 8]], A.is_ge, 0.0, 7, -1), ["cm1"], ["cm0"], 16)
    gc(lambda: g.affine_select(T.idn[:], T.ones[:], [[-1, 128]], A.is_equal, 0.0, 0, 1), ["ones"], ["idn"], 128)
    gc(lambda: g.iota(T.pf[:], [[1, 2], [0, 8], [2, 8]], 0, 0, allow_small_or_imprecise_dtypes=True), [], ["pf"], 128)
    for p0 in range(2):
        for c0 in range(2):
            o = 64 * p0 + 32 * c0
            gc(lambda o=o, c0=c0: g.iota(T.cf[:, o:o + 32], [[4, 2], [2, 2], [0, 8]], c0, 0, allow_small_or_imprecise_dtypes=True), [], ["cf%d" % o], 32)
    for z in ("wz", "uz", "w2z", "nwz"):
        if z in ("w2z", "nwz") and "V" not in ABS0 + ABS1:
            continue
        v(lambda z=z: V.memset(T[z][:], 0.0), [], [z], 144, 0.5)
    v(lambda: V.tensor_copy(T.wf[:], T.wti[:]), ["wti"], ["wf"], 1)
    v(lambda: V.tensor_scalar(T.wz[:, 15:143:16], T.bl[:, 0:128:16], T.wf[:, 0:1], None, A.mult), ["bl", "wf", "wz"], ["wz"], 8)
    if "V" in ABS0 + ABS1:
        v(lambda: V.tensor_scalar(T.w2z[:, 15:143:16], T.bl[:, 0:128:16], T.wf[:, 0:1], 2.0, A.mult, A.mult), ["bl", "wf"], ["w2z"], 8)
        v(lambda: V.tensor_scalar(T.nwz[:, 15:143:16], T.bl[:, 0:128:16], T.wf[:, 0:1], -1.0, A.mult, A.mult), ["bl", "wf"], ["nwz"], 8)
    v(lambda: V.tensor_scalar(T.uz[:, 15:143:16], T.bl[:, 0:128:16], 1.0, None, A.mult), ["bl"], ["uz"], 8)
    v(lambda: V.tensor_scalar(T.wb[:], T.bl[:], T.wf[:, 0:1], None, A.mult), ["bl", "wf"], ["wb"], 128)
    v(lambda: V.tensor_scalar(T.nid[:], T.idn[:], -1.0, None, A.mult), ["idn"], ["nid"], 128)
    v(lambda: V.tensor_copy(T.idb[:], T.idn[:]), ["idn"], ["idb"], 128)
    v(lambda: V.tensor_copy(T.nib[:], T.nid[:]), ["nid"], ["nib"], 128)
    v(lambda: V.tensor_scalar(T.pid[:, 1:2], T.pid[:, 0:1], 15, None, A.bitwise_and), ["pid0"], ["pid1"], 1)
    v(lambda: V.tensor_scalar(T.pid[:, 2:3], T.pid[:, 0:1], 7, None, A.bitwise_and), ["pid0"], ["pid2"], 1)
    v(lambda: V.tensor_copy(T.j16[:], T.pid[:, 1:2]), ["pid1"], ["j16"], 1)
    v(lambda: V.tensor_scalar(T.j8[:, 0:1], T.pid[:, 2:3], 8.0, None, A.subtract), ["pid2"], ["j8a"], 1)
    v(lambda: V.tensor_scalar(T.j8[:, 1:2], T.pid[:, 2:3], 16.0, None, A.subtract), ["pid2"], ["j8b"], 1)
    cfs = ["cf0", "cf32", "cf64", "cf96"]
    for k in range(2):
        v(lambda k=k: V.tensor_scalar(T.sel[:, k, :], T.cf[:], 8.0 * k, T.j16[:, 0:1], A.add, A.is_equal), cfs + ["j16"], ["sel%d" % k], 128)
    v(lambda: V.tensor_scalar(T.sel[:, 2, :], T.pf[:], T.j16[:, 0:1], None, A.is_equal), ["pf", "j16"], ["sel2"], 128)
    v(lambda: V.tensor_scalar(T.exl[:, 0:16], T.cm[:, 0, :], T.j8[:, 0:1], 8.0, A.mult, A.add), ["cm0", "j8a"], ["exl"], 16)
    v(lambda: V.tensor_scalar(T.exl[:, 16:32], T.cm[:, 0, :], T.j8[:, 1:2], 16.0, A.mult, A.add), ["cm0", "j8b"], ["exy0"], 16)
    v(lambda: V.tensor_scalar(T.exl[:, 32:40], T.bl[:, 0:128:16], T.j8[:, 0:1], 16.0, A.mult, A.add), ["bl", "j8a"], ["exy1"], 8)
    for h in range(2):
        v(lambda h=h: V.memset(T["sf%d" % h][:], 0.0), [], ["sfz%d" % h], 72)
    v(lambda: V.tensor_scalar(T.thp[:, 0:1], T.thi[:], 4080, None, A.bitwise_and), ["thi"], ["thp0"], 1)
    v(lambda: V.tensor_scalar(T.thp[:, 1:2], T.thi[:], 15, None, A.bitwise_and), ["thi"], ["thp1"], 1)
    v(lambda: V.tensor_scalar(T.thq[:], T.thp[:], -1.0, None, A.mult), ["thp0", "thp1"], ["thq"], 2)
    for k in range(2):
        v(lambda k=k: V.tensor_scalar(T.dth[:, k, :], T.idn[:], T.thq[:, k:k + 1], None, A.mult), ["idn", "thq"], ["dth%d" % k], 128)
    v(lambda: V.memset(T.onb[:], 1.0), [], ["onb"], 64)
    v(lambda: V.memset(T.bias[:, 0:128], -16.0), [], ["bias"], 128)
    v(lambda: V.memset(T.bias[0:1, 0:128], -15.5), [], ["bias"], 128)
    v(lambda: V.memset(T.bias[:, 128:256], -0.05859375), [], ["bias7"], 128)
    v(lambda: V.tensor_scalar(T.j7[:], T.j16[:], -1.0, 7.5, A.mult, A.add), ["j16"], ["j7"], 1)
    v(lambda: V.memset(T.rs[:], 1.0), [], ["rs"], 9)
    v(lambda: V.memset(T.oh0[:], 0.0), [], ["oh0", "ohc0"], 9)
    v(lambda: V.memset(T.bf0[:, 128:132], 0.0), [], ["bfz0"], 4)
    v(lambda: V.memset(T.bf1[:, 128:132], 0.0), [], ["bfz1"], 4)
    v(lambda: V.memset(T.ch[:, :, 128:132], 1.0), [], ["chz"], 8)

    def fromraw(x, outs, wname):
        rr = ["raw%d_%d" % (x, c) for c in range(8)]
        for qd in range(4):
            p0, c0 = qd >> 1, qd & 1
            v(lambda qd=qd, p0=p0, c0=c0: V.tensor_copy(outs(qd), T.raw[:, x, 4 * c0:4 * c0 + 4, p0::2]), rr, [wname % qd], 32)

    def half(t, h):
        H = str(h)
        cur[0] = 2 * t + h

        def n(*a):
            return [x + "@" + H for x in a]

        def tb(name):
            return T[name + H]
        ps = [T["ps%d%d" % (h, b)] for b in range(4)]
        ne = len(engs)
        win0 = T.xx[:, 0:4096]
        wins, wk = [T.xx[:, 0:8192]] * 4, [["xa", "xb"]] * 4
        lb = tb("lb")
        nl = tb("nl")
        if t == 0:
            fromraw(h, lambda qd: lb[:, 0, 32 * qd:32 * qd + 32], "lb0%d_" % h + "%d")
            if h == 0:
                for k in range(2):
                    fromraw(2 + k, lambda qd, k=k: T.ch[:, k, 32 * qd:32 * qd + 32], "chi%d_" % k + "%d")
        LB = ["lb%d%d_%d" % (t, h, qd) for qd in range(4)]
        cur[1] = 0

        f0, d0, z0 = tb("f0"), tb("d0"), tb("z0")
        s(lambda: S.activation(f0[:, 0, :], win0.indirect(lb[:, t, 0:32]), AF.Copy), ["xa", LB[0]], n("f0_0"), 512, GEST)
        if DGATH == "V":
            vg(lambda: V.tensor_copy(f0[:, 1, :], win0.indirect(lb[:, t, 96:128])), ["xa", LB[3]], n("f0_1"), 512)
        else:
            s(lambda: S.activation(f0[:, 1, :], win0.indirect(lb[:, t, 96:128]), AF.Copy), ["xa", LB[3]], n("f0_1"), 512, GEST)
        for reg, qd, y in (((2, 1, 0), (0, 2, 0)) if L0PE else ((2, 1, 0), (0, 2, 0), (1, 1, 1), (3, 2, 1))):
            vg(lambda reg=reg, qd=qd, y=y: V.tensor_tensor(d0[:, reg, :], win0.indirect(lb[:, t, 32 * qd:32 * qd + 32]), f0[:, y, :], A.subtract),
               ["xa", LB[qd]] + n("f0_%d" % y), n("d0_%d" % reg), 512)
        for reg, src, b in (((1, 2, 2), (3, 0, 3)) if L0PE else ()):
            pe([lambda b=b: P.matmul(ps[b][:, 0:512], T.idb[:], f0[:, 0, :], True, False),
                lambda b=b: P.matmul(ps[b][:, 0:512], T.nib[:], f0[:, 1, :], False, False),
                lambda b=b, src=src: P.matmul(ps[b][:, 0:512], T.idb[:], d0[:, src, :], False, True)],
               ["idb", "nib"] + n("f0_0", "f0_1", "d0_%d" % src), n("ps%d" % b), 512)

        for reg in ((2, 0) if L0PE else range(4)):
            s(lambda reg=reg: S.activation(z0[:, reg, :], d0[:, reg, :], AF.Abs), n("d0_%d" % reg), n("z0_%d" % reg), 512)
        for reg, b in (((1, 2), (3, 3)) if L0PE else ()):
            s(lambda reg=reg, b=b: S.activation(z0[:, reg, :], ps[b][:, 0:512], AF.Abs), [], n("ps%d" % b, "z0_%d" % reg), 512)

        def wsum(out, parts, bank, keys, per_r, to=lambda r: r):
            pe([lambda: P.matmul(out, T.bias[:, 0:128], T.onb[:, 0:per_r], True, False)], ["bias", "onb"], n(bank), per_r)
            fns = []
            for lz, f in parts:
                for r in range(16):
                    fns.append(lambda lz=lz, f=f, r=r: P.matmul(out, T[lz][:, 15 - to(r):143 - to(r)], f(r), False, r == 15))
            pe(fns, [p[0] for p in parts] + keys, n(bank), per_r)

        def index(iv, src, bank, m, mkey, nn):
            i = mkey
            tmp = ps[int(bank[2])][:, 384:384 + nn]
            v(lambda: V.tensor_scalar(iv[:, 0, :], src, M12, M12, A.add, A.subtract), [], n(bank, i + "0"), nn)
            v(lambda: V.tensor_scalar(tmp, src, 2639.5, None, A.add), [], n(bank, "t" + bank), nn)
            v(lambda: V.tensor_tensor(iv[:, 1, :], tmp, iv[:, 0, :], A.subtract), n(i + "0", "t" + bank), n(bank, i + "1"), nn)
            v(lambda: V.tensor_tensor(iv[:, 3, :], iv[:, 1, :], iv[:, 1, :], A.mult), n(i + "1"), n(i + "3"), nn, 2)
            v(lambda: V.tensor_scalar(m, iv[:, 3, :], 5, 4095, A.arith_shift_right, A.bitwise_and), n(i + "3"), n(i), nn)

        def tolist(out, in_, k, mkey, w, nn):
            v(lambda: V.tensor_scalar(out, in_, (KAP[k] - 10952) % 4096, None, A.add), n(mkey), n(w), nn)

        for a, b, kk in ((0, 2, "c"), (2, 4, "r")):
            bank = "ps0" if kk == "c" else "ps1"
            out = ps[0][:, 0:64] if kk == "c" else ps[1][:, 0:64]
            wsum(out, [("wz", lambda r, a=a, b=b: z0[:, a:b, r::16])], bank, n("z0_%d" % a, "z0_%d" % (a + 1)), 64)
            m = tb("m" + kk)
            index(tb("iv" + kk), out, bank, m[:], "m" + kk, 64)
            if kk == "c":
                tolist(nl[:, 0:32], m[:, :, 0], 0, "mc", "n1ec", 32)
                tolist(nl[:, 64:96], m[:, :, 1], 0, "mc", "n1oc", 32)
            else:
                tolist(nl[:, 32:64], m[:, :, 0, :], 0, "mr", "n1er", 32)
                tolist(nl[:, 96:128], m[:, :, 1, :], 0, "mr", "n1or", 32)
        f1, d1, z1 = tb("f1"), tb("d1"), tb("z1")
        for y, kk in ((0, "c"), (1, "r")):
            for z in range(NP1):
                w = 512 // NP1
                c0, c1, o = z * w, z * w + w, 32 * y + z * w // 16
                s(lambda y=y, c0=c0, c1=c1, o=o, w=w: S.activation(f1[:, y, c0:c1], wins[0].indirect(nl[:, o:o + w // 16]), AF.Copy),
                  wk[0] + n("n1e" + kk), n("f1%s%d" % (kk, z)), w, GEST)
                vg(lambda y=y, c0=c0, c1=c1, o=o, w=w: V.tensor_tensor(d1[:, y, c0:c1], wins[0].indirect(nl[:, 64 + o:64 + o + w // 16]), f1[:, y, c0:c1], A.subtract),
                   wk[0] + n("n1o" + kk, "f1%s%d" % (kk, z)), n("d1%s%d" % (kk, z)), w)
                if z == NP1 - 1 or y == 1:
                    c0 = 0 if y == 0 else c0
                    dk = n(*["d1%s%d" % (kk, x) for x in (range(NP1) if y == 0 else [z])])
                    s(lambda y=y, c0=c0, c1=c1: S.activation(d1[:, y, c0:c1], d1[:, y, c0:c1], AF.Abs), dk, dk, c1 - c0)
        wsum(ps[2][:, 0:64], [("wz", lambda r: d1[:, :, r::16])], "ps2", n(*["d1%s%d" % (x, z) for x in "cr" for z in range(NP1)]), 64)
        m1 = tb("m1")
        index(tb("iv1"), ps[2][:, 0:64], "ps2", m1[:], "m1", 64)
        tolist(nl[:, 128:144], m1[:, 0:2, :, 0::2], 1, "m1", "n2ec", 16)
        tolist(nl[:, 144:160], m1[:, 2:4, 0, :], 1, "m1", "n2er", 16)
        tolist(nl[:, 160:176], m1[:, 0:2, :, 1::2], 1, "m1", "n2oc", 16)
        tolist(nl[:, 176:192], m1[:, 2:4, 1, :], 1, "m1", "n2or", 16)
        f2, d2 = tb("f2"), tb("d2")
        d2k = []
        for y in range(NP2):
            w, yk = 512 // NP2, ["c"] if NP2 == 2 and y == 0 else ["r"] if NP2 == 2 else ["c", "r"]
            c0, c1, o = y * w, y * w + w, 128 + y * w // 16
            s(lambda c0=c0, c1=c1, o=o, w=w: S.activation(f2[:, c0:c1], wins[1].indirect(nl[:, o:o + w // 16]), AF.Copy),
              wk[1] + n(*["n2e" + x for x in yk]), n("f2%d" % y), w, GEST)
            vg(lambda c0=c0, c1=c1, o=o, w=w: V.tensor_tensor(d2[:, c0:c1], wins[1].indirect(nl[:, 32 + o:32 + o + w // 16]), f2[:, c0:c1], A.subtract),
               wk[1] + n("f2%d" % y, *["n2o" + x for x in yk]), n("d2%d" % y), w)
            s(lambda c0=c0, c1=c1: S.activation(d2[:, c0:c1], d2[:, c0:c1], AF.Abs), n("d2%d" % y), n("d2%d" % y), w)
            d2k += n("d2%d" % y)
        wsum(ps[0][:, 0:32], [("wz", lambda r: d2[:, r::16])], "ps0", d2k, 32, lambda r: 2 * (r % 8) + r // 8)
        iv2 = tb("iv2")
        index(iv2, ps[0][:, 0:32], "ps0", iv2[:, 4, :], "m2", 32)
        tolist(nl[:, 200:216], iv2[:, 4, 16:32], 2, "m2", "n3r", 16)
        tolist(nl[:, 192:200], iv2[:, 4, 0:16:2], 2, "m2", "n3e", 8)
        tolist(nl[:, 216:224], iv2[:, 4, 1:16:2], 2, "m2", "n3o", 8)
        f3, d3c, d3r, a3 = tb("f3"), tb("d3c"), tb("d3r"), tb("a3")
        s(lambda: S.activation(f3[:, 0:128], wins[2].indirect(nl[:, 192:200]), AF.Copy), wk[2] + n("n3e"), n("f3c"), 128, GEST)
        s(lambda: S.activation(f3[:, 128:384], wins[2].indirect(nl[:, 200:216]), AF.Copy), wk[2] + n("n3r"), n("f3r"), 256, GEST)
        vg(lambda: V.tensor_tensor(d3c[:], wins[2].indirect(nl[:, 216:224]), f3[:, 0:128], A.subtract), wk[2] + n("n3o", "f3c"), n("d3c"), 128)
        v(lambda: V.tensor_tensor(d3r[:], f3[:, 128:384:2], f3[:, 129:384:2], A.subtract), n("f3r"), n("d3r"), 128, 2)
        for y in range(2):
            s(lambda y=y: S.activation(a3[:, 0, :, y, :], d3c[:, y:128:2], AF.Abs), n("d3c"), n("a3c%d" % y), 64)
        s(lambda: S.activation(a3[:, 1, :, :, :], d3r[:], AF.Abs), n("d3r"), n("a3r"), 128)
        wsum(ps[1][:, 0:16], [("wz", lambda r: a3[:, :, :, :, r::16])], "ps1", n("a3c0", "a3c1", "a3r"), 16)
        iv3 = tb("iv3")
        index(iv3, ps[1][:, 0:16], "ps1", iv3[:, 4, :], "m3", 16)
        tolist(nl[:, 224:240], iv3[:, 4, :], 3, "m3", "n4", 16)
        q3 = tb("q3")
        s(lambda: S.activation(q3[:, 0, :], wins[3].indirect(nl[:, 224:232]), AF.Copy), wk[3] + n("n4"), n("q30"), 128, GEST)
        vg(lambda: V.tensor_tensor(q3[:, 1, :], wins[3].indirect(nl[:, 232:240]), q3[:, 0, :], A.subtract), wk[3] + n("n4", "q30"), n("q31"), 128)
        s(lambda: S.activation(q3[:, 2, :], q3[:, 1, :], AF.Abs), n("q31"), n("q32"), 128)
        si, sf, oh, cu = tb("si"), tb("sf"), tb("oh"), tb("cu")
        pe([lambda: P.matmul(ps[0][:, 0:8], T.bias[:, 128:256], T.onb[:, 0:8], True, False)], ["bias7", "onb"], n("ps0"), 8)
        pe([lambda: P.matmul(ps[0][:, 0:8], T.wb[:], q3[:, 0, 0:8], False, True)], ["wb"] + n("q30"), n("ps0"), 8)
        v(lambda: V.tensor_scalar(si[:, 0:8], ps[0][:, 0:8], M4, M4, A.add, A.subtract), [], n("ps0", "di"), 8)
        v(lambda: V.tensor_scalar(si[:, 16:24], ps[0][:, 0:8], T.j7[:, 0:1], None, A.add), ["j7"], n("ps0", "da"), 8)
        v(lambda: V.tensor_tensor(oh[:, 1:9], si[:, 16:24], si[:, 0:8], A.is_equal), ["oh" + H] + n("da", "di"), n("oh"), 8)
        v(lambda: V.tensor_tensor_scan(cu[:], T.rs[:], oh[:], 0.0, A.mult, A.max), ["rs", "oh" + H, "ohc" + H] + n("oh"), n("cu"), 9)
        if h == 0:
            s(lambda: S.activation(T.oh1[:, 0:1], T.cu0[:, 8:9], AF.Copy), n("cu"), ["ohc1"], 1)
        v(lambda: V.tensor_tensor(sf[:, 0:8], cu[:, 1:9], cu[:, 0:8], A.subtract), n("cu") + ["sfz" + H], n("fo"), 8, 2)
        lt, ltt = tb("lt"), tb("ltt")
        s(lambda: S.activation(lt[:], sf[:, 0:16].indirect(T.exl[:, 0:16]), AF.Copy), ["exl", "sfz" + H] + n("fo"), n("lt"), 256, GEST)
        fns = []
        for kap in range(16):
            r = house(kap)
            fns.append(lambda kap=kap, r=r: P.matmul(ps[2][:, 0:24], T.uz[:, 15 - r:143 - r], q3[:, :, 8 * kap:8 * kap + 8], kap == 0, False))
        for k in range(2):
            fns.append(lambda k=k: P.matmul(ps[2][:, 16:24], T.dth[:, k, :], T.onb[:, 0:8], False, k == 1))
        pe(fns, ["uz", "dth0", "dth1", "onb"] + n("q30", "q31", "q32"), n("ps2"), 24)
        v(lambda: V.tensor_copy(si[:, 32:40], ps[2][:, 0:8]), [], n("ps2", "qi"), 8)
        v(lambda: V.tensor_scalar(si[:, 56:64], si[:, 32:40], 15, None, A.bitwise_and), n("qi"), n("qa"), 8)
        for y, cmp in ((0, A.is_ge), (1, A.is_lt)):
            v(lambda y=y, cmp=cmp: V.tensor_scalar(sf[:, 40 + 8 * y:48 + 8 * y], ps[2][:, 8:16], 0.0, 9000.0, cmp, A.mult), ["sfz" + H], n("ps2", "cw%d" % y), 8)
            v(lambda y=y: V.tensor_tensor(sf[:, 56 + 8 * y:64 + 8 * y], ps[2][:, 16:24], sf[:, 40 + 8 * y:48 + 8 * y], A.min), n("cw%d" % y) + ["sfz" + H], n("ps2", "dm%d" % y), 8)
        for y in range(2):
            v(lambda y=y: V.tensor_tensor(sf[:, 16 + 8 * y:24 + 8 * y], sf[:, 56 + 8 * y:64 + 8 * y], si[:, 56:64], A.is_gt), n("qa", "dm%d" % y) + ["sfz" + H], n("mw" + "cr"[y]), 8)
        qrt = T.qr[:, t, 8 * h:8 * h + 8]
        v(lambda: V.tensor_tensor(qrt, sf[:, 16:24], sf[:, 24:32], A.add), n("mwc", "mwr"), ["qr%d%d" % (t, h)], 8)
        ly = tb("ly")
        s(lambda: S.activation(ly[:, 0:256], sf[:, 16:40].indirect(T.exl[:, 16:32]), AF.Copy), ["exy0", "sfz" + H] + n("mwc", "mwr"), n("lyc"), 256, GEST)
        vg(lambda: V.tensor_copy(ly[:, 256:384], sf[:, 16:40].indirect(T.exl[:, 32:40])), ["exy1", "sfz" + H] + n("mwc", "mwr"), n("lyr"), 128)
        bf, xm, dl, b2 = tb("bf"), tb("xm"), tb("dl"), tb("b2")
        v(lambda: V.tensor_copy(bf[:, 0:128], lb[:, t, :]), LB, n("bf"), 128)
        bp = ps[0][:, 256:384]
        s(lambda: S.activation(bp, bf[:, 0:128], AF.Copy), n("bf"), n("ps0"), 128)
        CH = (["chi%d_%d" % (k, qd) for k in range(2) for qd in range(4)] if t == 0 else []) + ["ch", "chz"]
        pe([lambda: P.matmul(ps[3][:, 0:129], T.nid[:], bf[:, 0:129], True, False)], ["nid", "bfz" + H] + n("bf"), n("ps3"), 129, 4)
        pe([lambda k=k: P.matmul(ps[3][:, 0:129], lt[:, 128 * k:128 * k + 128], T.ch[:, k, 0:129], False, k == 1) for k in range(2)],
           CH + n("lt"), n("ps3"), 129, 4)
        pe([lambda k=k: P.matmul(ps[1][:, 0:128], ly[:, 128 * k:128 * k + 128], T.sel[:, k, :], k == 0, k == 2) for k in range(3)],
           ["sel0", "sel1", "sel2"] + n("lyc", "lyr"), n("ps1"), 128)
        v(lambda: V.tensor_scalar(xm[:], ps[1][:, 0:128], 1.0, ps[3][:, 128:129], A.is_equal, A.mult), [], n("ps1", "ps3", "xm"), 128)
        v(lambda: V.tensor_tensor(dl[:], ps[3][:, 0:128], xm[:], A.mult), n("xm"), n("ps3", "dl"), 128)
        if t < ROUNDS - 1:
            v(lambda: V.tensor_tensor(b2[:], bp, dl[:], A.add), n("dl"), n("ps0", "b2"), 128)
            sn = tb("sn")
            v(lambda: V.tensor_copy(sn[:, t, :], b2[:]), n("b2"), n("sn%d" % t), 128)
            rid, pid = topo.addr(dst)[0:2]
            msk = sum(1 << e for e in engs)
            nxt = T["lb" + H][:, t + 1, :]
            rsem = T.sem["rc%d%d" % (t + 1, h)]
            op("G", [lambda: g.remote_dma(nxt, sn[:, t, :], rsem, T.sem.snd, pid, rid, msk)],
               n("sn%d" % t), ["sent%d%d" % (t, h)], 0.3, grp="send")
            op("N", [], ["sent%d%d" % (t, h)], ["lb%d%d_%d" % (t + 1, h, qd) for qd in range(4)], 2.0, sem=("rc%d%d" % (t + 1, h), ne))
        else:
            rob = tb("rob")
            for qd in range(4):
                p0, c0 = qd >> 1, qd & 1
                v(lambda qd=qd, p0=p0, c0=c0: V.tensor_tensor(rob[:, 4 * c0:4 * c0 + 4, p0::2], bp[:, 32 * qd:32 * qd + 32], dl[:, 32 * qd:32 * qd + 32], A.add),
                  n("dl"), n("ps0", "rob%d" % qd), 32)
            for c in range(8):
                q = "YS"[c % 2] if h else "Y"
                load(q, T.yb[c::8, 128 * h:128 * h + 128], rob[:, beta(c), :], ["yb%d%d" % (h, c)], "ost", n(*["rob%d" % (2 * x + (c & 1)) for x in range(2)]))
        pe([lambda k=k: P.transpose(ps[2][:, 128 * k:128 * k + 128], lt[:, 128 * k:128 * k + 128], T.idn[:]) for k in range(2)], ["idn"] + n("lt"), n("ps2"), 128, 4)
        s(lambda: S.activation(ltt[:], ps[2][:, 0:256], AF.Copy), [], n("ps2", "ltt"), 256)
        if h == 0:
            return
        both = [(k, y) for k in range(2) for y in range(2)]
        pe([lambda k=k, y=y: P.matmul(ps[2][:, 256 + 128 * k:384 + 128 * k], T["ltt%d" % y][:, 128 * k:128 * k + 128], T["dl%d" % y][:], y == 0, y == 1) for k, y in both],
           ["ltt@0", "dl@0"] + n("ltt", "dl"), n("ps2"), 128, 4)
        if t < ROUNDS - 1:
            v(lambda: V.tensor_tensor(T.ch[:, :, 0:128], T.ch[:, :, 0:128], ps[2][:, 256:512], A.subtract),
              CH, n("ps2") + ["ch"], 256)
        else:
            for qd in range(4):
                p0, c0 = qd >> 1, qd & 1
                u = [ps[2][:, 256 + 128 * k + 32 * qd:288 + 128 * k + 32 * qd] for k in range(2)]
                for k in range(2):
                    v(lambda qd=qd, p0=p0, c0=c0, k=k, u=u: V.tensor_tensor(T.roc[:, k, 4 * c0:4 * c0 + 4, p0::2], T.ch[:, k, 32 * qd:32 * qd + 32], u[k], A.subtract),
                      CH, n("ps2") + ["roc%d_%d" % (k, qd)], 32)
            for k in range(2):
                for c in range(8):
                    load("YS"[c % 2], T.yc[8 * k + c::16, :], T.roc[:, k, beta(c), :], ["yc%d%d" % (k, c)], "ost", ["roc%d_%d" % (k, 2 * x + (c & 1)) for x in range(2)])

    engs = topo.engines(core, dst)[::2]
    for t in range(ROUNDS):
        for h in range(2):
            half(t, h)
            cur[1] = None
    pe([lambda t=t: P.matmul(T.ps00[:, 256:272], T.idb[:], T.qr[:, t, :], t == 0, t == ROUNDS - 1) for t in range(ROUNDS)],
       ["idb"] + ["qr%d%d" % (t, h) for t in range(ROUNDS) for h in range(2)], ["ps0@0"], 16)
    s(lambda: S.activation(T.yqs[:], T.ps00[:, 256:272], AF.Copy), [], ["ps0@0", "yqs"], 16)
    load("Y", T.yq[:], T.yqs[:], ["yq"], "ost", ["yqs"])
    return ops, engs


def schedule(ops):
    nops = len(ops)
    succ = [[] for _ in range(nops)]
    for i, o in enumerate(ops):
        for d in o["d"]:
            succ[d].append(i)
    prio = [0.0] * nops
    for i in range(nops - 1, -1, -1):
        o = ops[i]
        prio[i] = o["c"] + o["lat"] + max([0.03 + prio[j] for j in succ[i]] or [0.0])
    for i, o in enumerate(ops):
        prio[i] = o.get("first", prio[i] - BIAS * o["b"] + OFFS * (o["b"] % 2) + TUNE.get(o["k"], 0.0))
    left = [len(o["d"]) for o in ops]
    ready = [0.0] * nops
    queues = ("V", "S", "P", "G", "Y", "N")
    free = {q: 0.0 for q in queues}
    cand = {q: set() for q in queues}
    for i in range(nops):
        if not left[i]:
            cand[ops[i]["q"]].add(i)
    order = []
    while True:
        best, bq = None, None
        for q in queues:
            if cand[q]:
                st = max(free[q], min(ready[j] for j in cand[q]))
                if best is None or st < best:
                    best, bq = st, q
        if bq is None:
            return order
        i = max((j for j in cand[bq] if ready[j] <= best), key=lambda j: prio[j])
        late = [j for j in cand[bq] if prio[j] > prio[i] and best < ready[j] < best + AHEAD * ops[i]["c"]]
        if late and bq != "N":
            j = min(late, key=lambda j: ready[j])
            fits = [k for k in cand[bq] if ready[k] + ops[k]["c"] <= ready[j] and ready[k] <= best]
            if fits:
                i = max(fits, key=lambda k: prio[k])
            else:
                free[bq] = ready[j]
                continue
        o = ops[i]
        cand[bq].remove(i)
        order.append(i)
        e = best + o["c"]
        if bq != "N":
            free[bq] = e
        e += o["lat"]
        o["t"] = (best, e)
        for j in succ[i]:
            left[j] -= 1
            ready[j] = max(ready[j], e + (EST["wl"] if ops[j]["q"] == bq else EST["wc"]))
            if not left[j]:
                cand[ops[j]["q"]].add(j)


def rank_program(g, core, T, topo):
    rank = T.rank_of(core)
    if rank is None:
        return
    ops, engs = build(g, core, T, topo)
    order = schedule(ops)
    queue = {"V": g.vector, "S": g.scalar, "P": g.tensor, "G": g, "Y": g.sync}
    total = {}
    for o in ops:
        if o["grp"] and o["grp"] != "send":
            total[o["grp"]] = total.get(o["grp"], 0) + 16
    known = {q: {} for q in queue}
    count = {}
    for i in order:
        o = ops[i]
        q = o["q"]
        if q == "N":
            o["tok"] = o["sem"]
            o["clk"] = {}
            continue
        kn = known[q]
        for d in sorted(o["d"], key=lambda d: -order.index(d) if False else -d):
            tok = ops[d].get("tok")
            if tok is None:
                continue
            if kn.get(tok[0], 0) < tok[1]:
                queue[q].wait_ge(T.sem[tok[0]], tok[1])
                kn[tok[0]] = tok[1]
                for a, b in ops[d]["clk"].items():
                    if kn.get(a, 0) < b:
                        kn[a] = b
        o["clk"] = dict(kn)
        if o["grp"] == "send":
            for f in o["f"]:
                f()
            o["tok"] = None
        elif o["grp"]:
            for f in o["f"]:
                f().then_inc(T.sem[o["grp"]], 16)
            o["tok"] = (o["grp"], total[o["grp"]])
        else:
            sem = "e" + q
            for f in o["f"]:
                f().then_inc(T.sem[sem], 1)
                count[sem] = count.get(sem, 0) + 1
            o["tok"] = (sem, count[sem])
    for sem in sorted(count):
        g.wait_ge(T.sem[sem], count[sem])
    for sem in sorted(total):
        g.wait_ge(T.sem[sem], total[sem])
    g.wait_ge(T.sem.snd, 2 * (ROUNDS - 1) * len(engs))
    for t in range(1, ROUNDS):
        for h in range(2):
            g.wait_ge(T.sem["rc%d%d" % (t, h)], len(engs))
